import numpy as np, ml_dtypes
CORES = [2,6,10,14,18,22,26,30]
N = 8
import mx_ref
BF = ml_dtypes.bfloat16
def gcols(t, e):
    v = np.concatenate([t.reshape(8, 16, -1, 4), np.zeros((8, 16, 1, 4), BF)], axis=2)
    return np.ascontiguousarray(np.stack([v[g][:, e[g]] for g in range(8)])).reshape(128, -1)
def tile(rs):
    return np.stack(rs, axis=2).reshape(128, -1).astype(BF)
def pick(q, e):
    c = np.concatenate([q[0].reshape(128, -1, 4), np.zeros((128, 1, 4), np.uint8)], axis=1); s = np.concatenate([q[1], np.ones((16, 1), np.uint8)], axis=1)
    return (np.ascontiguousarray(c[:, e].reshape(128, -1)), np.ascontiguousarray(s[:, e]))
def join(*qs):
    return (np.concatenate([q[0] for q in qs], axis=1), np.concatenate([q[1] for q in qs], axis=1))
def put(q, e, v):
    c, s = q[0].reshape(128, -1, 4).copy(), q[1].copy(); c[:, e] = v[0].reshape(128, -1, 4); s[:, e] = v[1]
    return (c.reshape(128, -1), s)
def pk(c, s):
    return (np.ascontiguousarray(c), mx_ref.live(s))
def emit(q):
    return q[0], q[1]
def packed(v, rng):
    q = [mx_ref.quantize(np.ascontiguousarray(v[r])) for r in range(N)]
    return np.stack([a for a, b in q]), np.stack([mx_ref.plane(b, rng) for a, b in q])
def values_of_codes():
    e, c = np.zeros((128, 128, 4), np.float32), np.zeros((128, 2, 4), np.uint8)
    e[np.arange(128), np.arange(128), 0] = 1
    c[:127, :, 0] = np.arange(256).reshape(2, 128).T[:127]
    return mx_ref.matmul(mx_ref.quantize(e.reshape(128, 512).astype(BF)), (c.reshape(128, 8), np.full((16, 2), 127, np.uint8))).T.reshape(-1).astype(np.float64)
CODE_VALUE, SCALE_VALUE = values_of_codes(), 2.0 ** (np.arange(256) - 127.0)
def decode(q):
    return (CODE_VALUE[q[0]].reshape(16, 8, -1, 4) * SCALE_VALUE[q[1]][:, None, :, None] + 0.0).reshape(128, -1).astype(np.float32)
def f(rng, *shape):
    return mx_ref.flush((rng.standard_normal(shape, dtype=np.float32) * np.exp2(rng.integers(-2, 3, shape[:-1] + (1,)))).astype(BF))
def wide(rng, *shape, cols=0):
    v = rng.standard_normal(shape, dtype=np.float32) * np.exp2(rng.integers(-12, 13, shape)).astype(np.float32)
    if cols: v *= np.repeat(np.exp2(rng.integers(-cols, cols + 1, shape[:-2] + (1, shape[-1] // 4))) * (rng.random(shape[:-2] + (1, shape[-1] // 4)) > 0.0625), 4, axis=-1).astype(np.float32)
    return mx_ref.flush(v.astype(BF))
C, H, M, R = 512, 6, 64, 2
def keys(p):
    b = p.reshape(8, 16, -1)[:, :H] > 0
    return np.sum(b * (1 << np.arange(H))[:, None], axis=1)
def cells(a, key):
    a = a.reshape(8, 16, C, 4)
    c = np.zeros((8, 16, M, 4), np.float32)
    for g in range(8):
        for k in np.unique(key[g]): c[g, :, k] = np.max(a[g][:, key[g] == k], axis=1)
    return c.reshape(128, 4 * M).astype(BF)
def big(v, k):
    v = v.astype(np.float32) * np.float32(k)
    v[np.abs(v) < np.float32(2.0 ** -16)] = 0
    return v.astype(BF)
def weights(rng, k, still=0):
    w = big(f(rng, 128, 2048), k).reshape(128, 4, 128, 4)
    w[:, :, np.arange(128) % 16 < still] = 0
    w = w.reshape(128, 2048)
    c, p = packed(np.stack([w] * N), rng)
    return {"wc": c, "ws": p}
def numbers_of(rng):
    return {"x": big(f(rng, N, 128, 4 * C), 1), "u": np.array(f(rng, N, 128, 512)), "v": np.array(f(rng, N, 128, 512))}
def aim(d, x, key, size):
    u = d["u"].reshape(N, 128, 128, 4)
    for i in range(H):
        x[:, :, i // 4, :, i % 4] = np.where((key >> i) & 1, size, -size)
        for g in range(8):
            u[:, :, 16 * g + i] = 0
            u[:, 16 * g + i // 4, 16 * g + i, i % 4] = 1
def setup_inputs(rng):
    return {**numbers_of(rng), **weights(rng, 1)}
def setup_inputs_ties(rng):
    d = numbers_of(rng)
    d["u"].reshape(N, 8, 16, 128, 4)[:, :, 8:] = 0
    x = d["x"].reshape(N, 8, 16, C, 4)
    e = rng.permutation(N)
    for r in range(N):
        a = x[r][:, :, :1].copy()
        k = rng.permutation(C) % 4
        if r == e[1]: k[:] = 2
        x[r][:, :, k == 0] = 0
        x[r][:, :8, k == 1] = 0
        x[r][:, :, k == 2] = a
    x[e[0]] = 0
    return {**d, "x": x.reshape(N, 128, 4 * C), **weights(rng, 1)}
def setup_inputs_near(rng):
    d = numbers_of(rng)
    x = rng.integers(4, 8, (N, 8, 16, C, 4)) * rng.choice([-0.25, 0.25], (N, 8, 16, C, 4))
    x[:, :, :8] = 0
    s = rng.choice([-1.0, 1.0], (N, 8, C))
    x[:, :, 8, :, 0] = s
    x[:, :, 9, :, 0] = -s
    o = rng.permutation(N)
    a = int(np.argmax(o == 1))
    x[a, :, 8:10, :, 0] = 0
    x[a, :, 7, :, 0] = -s[a] * 2.0 ** -27
    k = np.where(o % 2 == 0, 1.0, 2.0 ** -30).astype(np.float32).astype(BF)
    u = d["u"].reshape(N, 128, 128, 4)
    for i in range(H):
        c = rng.choice([-1.0, 0.0, 1.0, 1.0], (N, 8, C))
        x[:, :, i // 4, :, i % 4] = c * 2.0 ** -23
        x[a, :, i // 4, :, i % 4] = (s[a] + c[a] * 0.125) * 2.0 ** -27
        for g in range(8):
            u[:, :, 16 * g + i] = 0
            u[:, 16 * g + i // 4, 16 * g + i, i % 4] = k
            u[:, 16 * g + 7:16 * g + 10, 16 * g + i, 0] = k[:, None]
    return {**d, "x": x.astype(np.float32).reshape(N, 128, 4 * C).astype(BF), **weights(rng, 1, 10)}
def setup_inputs_huge(rng):
    d = numbers_of(rng)
    key = np.stack([np.stack([rng.permutation(C) % M for g in range(8)]) for r in range(N)])
    sign = np.stack([rng.permutation(M) % 2 * 2.0 - 1.0 for g in range(8)])
    size = rng.integers(8, 17, (N, 8, 16, C, 4))
    size[..., :2] = 16
    x = size * 2.0 ** 26 * sign[np.arange(8)[:, None], key][:, :, None, :, None]
    aim(d, x, key, 2.0 ** 30)
    d["u"] = big(d["u"], 2.0 ** 25)
    return {**d, "x": x.astype(np.float32).reshape(N, 128, 4 * C).astype(BF), **weights(rng, 2.0 ** -3, 2)}
def setup_inputs_crowd(rng):
    d = numbers_of(rng)
    e = rng.permutation(N)
    half = rng.permutation(8) < 4
    nil = rng.permutation(8) < 2
    p = int(e[3]) * (M // N) + M // N - 2
    gone = rng.choice([r for r in range(1, N) if r != e[3]])
    there = np.array([k for k in range(M) if k // (M // N) != gone and k not in (p, p + 1)])
    j = rng.permutation(C)
    key, low = np.zeros((N, 8, C), int), np.zeros((N, 8, C), bool)
    for g in range(8):
        c = rng.permutation(there)
        if nil[g]: c = np.concatenate([[0], c[c != 0]])
        for r in range(N):
            k = np.concatenate([c[:1], rng.choice(c[2:], C - 1)])
            if r == e[1] or r == e[0] and half[g]: k[:] = c[0]
            if r == e[2]: k = np.resize(c, C)
            if r == e[3]: key[r, g, j] = np.concatenate([[p, p + 1, p + 1], rng.permutation(k[:-3])])
            else: key[r, g] = rng.permutation(k)
        low[:, g] = (key[:, g] == c[0]) | (key[:, g] == c[1])
    x = d["x"].astype(np.float32).reshape(N, 8, 16, C, 4)
    x = np.where(low[:, :, None, :, None], -1 - np.abs(x), x)
    a = x[e[1]]
    a[:, 2:, 0, 1] = 0
    a[:, 2:, -1, 2] = 0
    b = x[e[3]]
    b[:, 8:, j[0]] = (1 + rng.random((8, 8, 4))) * np.exp2(rng.integers(-1, 4, (8, 8, 4)))
    b[:, 15, j[0], 3] = -127 * 2.0 ** 10
    b[:, 8:, j[1]] = 1 + rng.random((8, 8, 4))
    b[:, 15, j[1], 3] = -2.0 ** 22
    b[:, 8:, j[2]] = -1 - rng.random((8, 8, 4))
    aim(d, x, key, 1.0)
    a[nil, :, -1] = 0
    return {**d, "x": x.astype(np.float32).reshape(N, 128, 4 * C).astype(BF), **weights(rng, 1, 2)}
def setup_inputs_spread(rng):
    d = setup_inputs(rng)
    d["x"] = big(wide(rng, N, 128, 4 * C, cols=6), 1)
    return d
def check_inputs(d):
    b = []
    for k in ("x", "u", "v"):
        a = np.abs(d[k].astype(np.float32))
        if not (np.isfinite(a).all() and ((a == 0) | (a >= 2.0 ** -30) & (a <= 2.0 ** 30)).all()): b.append("a value of " + k)
    if (d["wc"] != d["wc"][:1]).any(): b.append("wc differs between ranks")
    s = [mx_ref.live(p) for p in d["ws"]]
    if any((p != s[0]).any() for p in s): b.append("ws differs between ranks")
    try:
        a = np.abs(decode(pk(d["wc"][0], d["ws"][0])))
        m = np.max(a.reshape(16, 8, 512, 4), axis=(1, 3))
        good = bool(np.isfinite(a).all() and ((m == 0) | (m >= 2.0 ** -30) & (m <= 2.0 ** 30)).all())
    except Exception:
        good = False
    if not good: b.append("a value of W")
    return b
def reference(x, u, v, wc, ws):
    w = pk(wc[0], ws[0])
    qu = [mx_ref.quantize(u[r]) for r in range(N)]
    now = [x[r] for r in range(N)]
    kl = np.zeros((N, 8 * R, C), np.float32)
    for t in range(R):
        held, key, made = [], [], []
        for r in range(N):
            q = mx_ref.quantize(now[r])
            key.append(keys(mx_ref.matmul(qu[r], q)))
            held.append(decode(q))
            made.append(mx_ref.quantize(cells(held[r], key[r])))
            kl[r, 8 * t:8 * t + 8] = key[r]
        merged = np.max(decode(join(*made)).reshape(128, N, 4 * M), axis=1)
        z = mx_ref.quantize(np.ascontiguousarray(merged.astype(BF)))
        g = tile([np.maximum(mx_ref.matmul(pick(w, np.arange(128 * b, 128 * b + 128)), z), np.float32(0.0)) * np.float32(0.015625) for b in range(4)])
        back = decode(mx_ref.quantize(g)).astype(BF)
        for r in range(N):
            now[r] = ((held[r] + gcols(back, key[r]).astype(np.float32)) * np.float32(0.5)).astype(BF)
    y = np.zeros((N, 128, C), np.float32)
    oc, osc = np.zeros((N, 128, 4 * C), np.uint8), np.zeros((N, 16, C), np.uint8)
    for r in range(N):
        q = mx_ref.quantize(now[r])
        y[r] = mx_ref.matmul(mx_ref.quantize(v[r]), q)
        oc[r], osc[r] = emit(q)
    return {"y": y, "kl": kl, "oc": oc, "osc": osc}

@@ -1,0 +1,539 @@
+from concourse.bass import DstId, RemoteDMATransfer
+from concourse.mybir import dt, AluOpType, AxisListType, ActivationFunctionType
+
+OP, ACT, AX = AluOpType, ActivationFunctionType, AxisListType
+ROUNDS = 2
+BIG = 2.0 ** 60
+MAGIC = 1.5 * 2.0 ** 27
+GV = 5
+
+SCRATCH = {}
+
+
+def _b(names, n, dtype="bfloat16"):
+    for name in names.split():
+        SCRATCH[name] = ("sbuf", [128, n], dtype)
+
+
+def _codes(names, n):
+    for name in names.split():
+        SCRATCH[name] = ("sbuf", [128, n], "float8_e4m3fn_x4")
+        SCRATCH[name + "s"] = ("sbuf", [128, n], "uint8")
+
+
+_b("xs st1 st2 ebt dd sd ge", 2048)
+_b("us vs bt at zt gt vals lo lsw ltr sj m8", 512)
+_b("in2 in3 is2 is3", 512)
+_b("one nul idm krm upd lod prm", 128)
+_b("gw0 gw1 gw2", 8)
+_b("kc", 66)
+_b("ktt", 1680)
+_b("lt", 4096)
+_b("prt", 1792)
+_b("ot", 2080)
+_b("tt", 560)
+_b("msk0 msk1", 592)
+_b("sc", 2304)
+_b("neg", 64)
+_b("own mm gb", 256)
+_b("rw rv", 140, "float32")
+_b("kf yb", 512, "float32")
+_b("lj lk", 32, "float32")
+_b("acc b5 cneg tb", 5, "float32")
+_b("em dm mk pk dum c16", 4, "float32")
+_b("icf icb", 1, "float32")
+_b("ip ia", 1, "int32")
+_b("po ko l16", 32, "uint16")
+_b("mk16 pk16", 4, "uint16")
+_codes("qu qv qb qa0 qa1 qz qg", 128)
+_codes("qx0 qx1 qx2 qw qe qh qr", 512)
+_codes("qk", 420)
+_codes("ql", 1024)
+_codes("qp", 448)
+_codes("qo", 520)
+_codes("qt", 140)
+_codes("lc0 lc1", 448)
+for _i in range(8):
+    SCRATCH["ps%d" % _i] = ("psum", [128, 512], "float32")
+
+SEMAPHORES = ["cv", "cs", "ct", "cq", "ar0", "ar1", "sent",
+              "dx0", "dx1", "du", "dv", "dwc", "dws", "dlo", "dk0", "dk1", "dy0", "dy1", "do0", "do1", "ds"]
+
+_MASKS = {}
+
+
+def _cols(a, b, st):
+    if (a, b, st) not in _MASKS:
+        m = 0
+        for i in range(a, b, st):
+            m |= 1 << i
+        _MASKS[(a, b, st)] = m
+    return _MASKS[(a, b, st)]
+
+
+def prog(g, T):
+    eng = {"v": g.vector, "s": g.scalar, "t": g.tensor, "q": g, "y": g.sync}
+    csem = {"v": "cv", "s": "cs", "t": "ct", "q": "cq"}
+    count = {s: 0 for s in SEMAPHORES}
+    known = {e: {} for e in eng}
+    snap = {}
+    wr, rd = {}, {}
+
+    def wait(e, sem, val):
+        if known[e].get(sem, 0) < val:
+            eng[e].wait_ge(T.sem[sem], val)
+            for s, k in snap.get((sem, val), {}).items():
+                if known[e].get(s, 0) < k:
+                    known[e][s] = k
+            known[e][sem] = val
+
+    def need(e, reads, writes):
+        n = {}
+
+        def add(tok):
+            if n.get(tok[0], 0) < tok[1]:
+                n[tok[0]] = tok[1]
+        for name, m in reads:
+            psum = name[:2] == "ps"
+            for wm, tok, we in wr.get(name, []):
+                if wm & m and not (psum and we == e):
+                    add(tok)
+            if psum:
+                for rm, tok, re_ in rd.get(name, []):
+                    if re_ != e:
+                        add(tok)
+        for name, m in writes:
+            for om, tok, oe in wr.get(name, []) + rd.get(name, []):
+                if om & m and not (e == "t" and oe == "t"):
+                    add(tok)
+        return n
+
+    def note(e, reads, writes, tok):
+        for name, m in writes:
+            wr[name] = [w for w in wr.get(name, []) if w[0] & ~m] + [(m, tok, e)]
+            rd[name] = [r for r in rd.get(name, []) if r[0] & ~m]
+        for name, m in reads:
+            rd[name] = [r for r in rd.get(name, [])
+                        if not (r[2] == e and e != "dma" and r[0] & ~m == 0)] + [(m, tok, e)]
+
+    def emit(e, call, reads, writes, sem=None):
+        n = need(e, reads, writes)
+        for s in sorted(n, key=lambda s: -n[s]):
+            wait(e, s, n[s])
+        s = sem or csem[e]
+        k = 16 if sem else 1
+        call().then_inc(T.sem[s], k)
+        count[s] += k
+        snap[(s, count[s])] = dict(known[e])
+        note("dma" if sem else e, reads, writes, (s, count[s]))
+    return eng, count, wait, emit, need
+
+
+def rank_program(g, core, T, topo):
+    rank = T.rank_of(core)
+    if rank is None:
+        return
+    N = len(T.cores)
+    eng, count, wait, emit, need = prog(g, T)
+    V, S, PE = g.vector, g.scalar, g.tensor
+
+    def R(name, a=0, b=None, st=1):
+        if name[:2] == "ps":
+            return (name, 1)
+        return (name, _cols(a, SCRATCH[name][1][1] if b is None else b, st))
+
+    def A(name, a=0, b=None, st=1):
+        b = SCRATCH[name][1][1] if b is None else b
+        return T[name][:, a:b] if st == 1 else T[name][:, a:b:st]
+
+    def both(x):
+        return A(*x), R(*x)
+
+    def fill(x, c):
+        a, r = both(x)
+        emit("v", lambda: V.memset(a, c), [], [r])
+
+    def vcopy(o, i):
+        (oa, orr), (ia, ir) = both(o), both(i)
+        emit("v", lambda: V.tensor_copy(oa, ia), [ir], [orr])
+
+    def vts(o, i, s1, s2, op0, op1=None, off=None):
+        (oa, orr), (ia, ir) = both(o), both(i)
+        rs = [ir]
+        if isinstance(s1, tuple):
+            s1, r1 = both(s1)
+            rs.append(r1)
+        if off:
+            fa, fr = both(off)
+            ia = ia.indirect(fa)
+            rs.append(fr)
+        if op1 is None:
+            emit("v", lambda: V.tensor_scalar(oa, ia, s1, None, op0), rs, [orr])
+        else:
+            emit("v", lambda: V.tensor_scalar(oa, ia, s1, s2, op0, op1), rs, [orr])
+
+    def vtt(o, i0, i1, op, off=None):
+        (oa, orr), (a0, r0), (a1, r1) = both(o), both(i0), both(i1)
+        rs = [r0, r1]
+        if off:
+            fa, fr = both(off)
+            a0 = a0.indirect(fa)
+            rs.append(fr)
+        emit("v", lambda: V.tensor_tensor(oa, a0, a1, op), rs, [orr])
+
+    def vscan(o, mask, data):
+        (oa, orr), (ma, mr), (da, dr) = both(o), both(mask), both(data)
+        emit("v", lambda: V.tensor_tensor_scan(oa, ma, da, -BIG, OP.min, OP.max), [mr, dr], [orr])
+
+    def vgather(o, i, off):
+        (oa, orr), (ia, ir), (fa, fr) = both(o), both(i), both(off)
+        emit("v", lambda: V.tensor_copy(oa, ia.indirect(fa)), [ir, fr], [orr])
+
+    def vscatter(o, i, off):
+        (oa, orr), (ia, ir), (fa, fr) = both(o), both(i), both(off)
+        emit("v", lambda: V.tensor_copy(oa.indirect(fa), ia), [ir, fr], [orr])
+
+    def vtrans(o, i):
+        (oa, orr), (ia, ir) = both(o), both(i)
+        emit("v", lambda: V.transpose(oa, ia), [ir], [orr])
+
+    def vmax(o, i):
+        (oa, orr), (ia, ir) = both(o), both(i)
+        emit("v", lambda: V.tensor_reduce(oa, ia, AX.X, OP.max), [ir], [orr])
+
+    def quant(q, a, b, x, xa, xb):
+        emit("v", lambda: V.quantize_mx(T[q][:, a:b], T[q + "s"][:, a:b], T[x][:, xa:xb]),
+             [R(x, xa, xb)], [R(q, a, b)])
+
+    def act(o, i, f, bias=0.0, scale=1.0, off=None, accum=None):
+        (oa, orr), (ia, ir) = both(o), both(i)
+        rs, ws = [ir], [orr]
+        if isinstance(bias, tuple):
+            bias, r1 = both(bias)
+            rs.append(r1)
+        if off:
+            fa, fr = both(off)
+            ia = ia.indirect(fa)
+            rs.append(fr)
+        if accum:
+            aa, ar = both(accum)
+            ws.append(ar)
+            emit("s", lambda: S.activation(oa, ia, f, bias=bias, scale=scale, accum_out=aa), rs, ws)
+        else:
+            emit("s", lambda: S.activation(oa, ia, f, bias=bias, scale=scale), rs, ws)
+
+    def mm(ps, n, w, wa, x, xa, start=True, stop=True):
+        emit("t", lambda: PE.matmul_mx(T[ps][:, 0:n], T[w][:, wa:wa + 128], T[w + "s"][:, wa:wa + 128],
+                                       T[x][:, xa:xa + n], T[x + "s"][:, xa:xa + n], start, stop),
+             [R(w, wa, wa + 128), R(w + "s", wa, wa + 128), R(x, xa, xa + n)], [R(ps)])
+
+    def dma(q, sem, oap, iap, reads, writes):
+        emit(q, lambda: eng[q].dma_start(oap, iap), reads, writes, sem=sem)
+
+    def sel(o, i, pattern, cmp, fillv, base, cm):
+        (oa, orr), (ia, ir) = both(o), both(i)
+        emit("q", lambda: g.affine_select(oa, ia, pattern, cmp, fillv, base, cm), [ir], [orr])
+
+    def iota(o, pattern, base, cm):
+        oa, orr = both(o)
+        if SCRATCH[o[0]][2] == "int32":
+            emit("q", lambda: g.iota(oa, pattern, base, cm), [], [orr])
+        else:
+            emit("q", lambda: g.iota(oa, pattern, base, cm, allow_small_or_imprecise_dtypes=True), [], [orr])
+
+    dma("y", "dx0", T.xs[:, 0:1024], T.x[:, 0:1024], [], [R("xs", 0, 1024)])
+    dma("s", "du", T.us[:, 0:512], T.u[:, 0:512], [], [R("us")])
+    dma("y", "dx1", T.xs[:, 1024:2048], T.x[:, 1024:2048], [], [R("xs", 1024, 2048)])
+    dma("y", "dwc", T.qw[:, 0:512].bitcast(dt.uint8), T.wc[:, 0:2048], [], [R("qw")])
+    dma("y", "dws", T.qws[:, 0:512], T.ws[:, 0:512], [], [R("qws")])
+    dma("y", "dv", T.vs[:, 0:512], T.v[:, 0:512], [], [R("vs")])
+
+    for n in ("gw0", "gw1", "gw2"):
+        fill((n,), 0.0)
+    fill(("one",), 1.0)
+    fill(("nul",), 0.0)
+    fill(("ktt",), 0.0)
+    fill(("krm",), 0.0)
+    fill(("ebt",), 0.0)
+    fill(("prt",), 0.0)
+    for i in range(6):
+        sel(("gw0",), ("gw0",), [[-16, 8]], OP.not_equal, 2.0 ** (i - 1), -i, 1)
+    for i in range(6):
+        w = "gw1" if i < 2 else "gw2"
+        sel((w,), (w,), [[-16, 8]], OP.not_equal, 8.0 * 2 ** i if i < 2 else 0.125 * 2 ** i, -i, 1)
+    sel(("idm",), ("one",), [[-1, 128]], OP.is_equal, 0.0, 0, 1)
+    iota(("kc", 0, 65), [[1, 65]], -32, 0)
+    sel(("upd",), ("one",), [[1, 128]], OP.is_gt, 0.0, 0, -1)
+    sel(("upd",), ("upd",), [[1, 128]], OP.not_equal, 1024.0, 0, -1)
+    sel(("lod",), ("one",), [[-1, 128]], OP.is_gt, 0.0, 0, 1)
+    sel(("lod",), ("lod",), [[-1, 128]], OP.not_equal, -1024.0, 0, 1)
+    sel(("prm",), ("one",), [[-1, 4], [-4, 32]], OP.is_equal, 0.0, 0, 1)
+    for i in range(6):
+        sel(("krm",), ("krm",), [[-16, 8], [0, 16]], OP.not_equal, 2.0 ** (i - 1), -i, 1)
+    iota(("ip",), [[0, 1]], 0, 1)
+    iota(("cneg",), [[-1, 5]], 0, 0)
+    iota(("c16",), [[16, 4]], 513, 0)
+    iota(("lo",), [[0, 2], [1, 256]], 0, 0)
+    iota(("vals",), [[256, 2], [0, 256]], 0, 0)
+    dma("y", "dlo", T.vals[1:128:16, :], T.lo[1:128:16, :], [R("lo")], [R("vals")])
+
+    def ones_and_zeros(cs):
+        for c in cs:
+            for b in range(4):
+                for s, o in ((0, b < c), (1, b > c)):
+                    if b != c:
+                        act(("lt", 2048 * s + 512 * c + b, 2048 * s + 512 * c + 512, 4), ("one" if o else "nul",), ACT.Copy)
+    ones_and_zeros((0, 1, 2))
+    for b in range(4):
+        for k in range(3):
+            act(("ktt", 560 * k + 48 + 5 * b, 560 * k + 560, 64), ("gw%d" % k,), ACT.Copy)
+    quant("qu", 0, 128, "us", 0, 512)
+    fill(("rw", 0, 12 + 16 * GV), 1287.5)
+    fill(("rw", 12 + 16 * GV, 140), 263.5)
+    fill(("m8",), BIG)
+    fill(("m8", 0, 512, 8), -BIG)
+
+    others = [r for r in range(N) if r != rank]
+    near = [r for r in others if topo.chip(T.cores[r]) == topo.chip(core)]
+    far = [r for r in others if r not in near]
+    fmask = topo.mask(core, T.cores[far[0]])
+    nmask = topo.mask(core, T.cores[near[0]]) & ~fmask
+    arrive = 0
+    for r in others:
+        arrive += 2 * bin(nmask if r in near else fmask).count("1")
+
+    def send(t):
+        qa, lc = "qa%d" % t, "lc%d" % t
+        n = need("q", [R(qa)], [])
+        for s in n:
+            wait("q", s, n[s])
+        for plane in (0, 1):
+            ts = []
+            for group, m in ((far, fmask), (near, nmask)):
+                ids, dsts = [], []
+                for r in group:
+                    rid, pid = topo.addr(T.cores[r])[:2]
+                    slot = rank - (1 if rank > r else 0)
+                    ids.append(DstId(rid=rid, pnc=pid))
+                    dsts.append(T[lc + "s"][:, 64 * slot:64 * slot + 64] if plane
+                                else T[lc][:, 64 * slot:64 * slot + 64].bitcast(dt.uint8))
+                src = T[qa + "s"][:, 0:64] if plane else T[qa][:, 0:64].bitcast(dt.uint8)
+                ts.append(RemoteDMATransfer(dst_ids=ids, dma_engine_mask=m, remote_sem=T.sem["ar%d" % t],
+                                            srcs=[src], dsts=dsts))
+                count["sent"] += bin(m).count("1")
+            g.remote_dma_fused(ts, local_sem=T.sem.sent)
+
+    def ps(i):
+        return "ps%d" % i
+    PC0, PC1 = [4, 5, 6, 7], [0, 1, 3, 2]
+    VR = 12 + 16 * GV
+
+    def key_half(t, state, h):
+        qx = "qx%d" % t
+        if h or not t:
+            quant(qx, 256 * h, 256 * h + 256, state, 1024 * h, 1024 * h + 1024)
+        if t < ROUNDS:
+            mm(ps(h), 256, "qu", 0, qx, 256 * h)
+            act(("bt", 256 * h, 256 * h + 256), (ps(h), 0, 256), ACT.Sign, bias=-(2.0 ** -100))
+        else:
+            mm(ps(h), 256, "qv", 0, qx, 256 * h)
+            act(("yb", 256 * h, 256 * h + 256), (ps(h), 0, 256), ACT.Copy)
+            dma("y", "do%d" % h, T.oc[:, 1024 * h:1024 * h + 1024], T[qx][:, 256 * h:256 * h + 256].bitcast(dt.uint8),
+                [R(qx, 256 * h, 256 * h + 256)], [])
+            dma("s", "dy%d" % h, T.y[:, 256 * h:256 * h + 256], T.yb[:, 256 * h:256 * h + 256],
+                [R("yb", 256 * h, 256 * h + 256)], [])
+
+    key_half(0, "xs", 0)
+    key_half(0, "xs", 1)
+    for b in range(4):
+        act(("ebt", 512 * b + b, 512 * b + 512, 4), ("idm",), ACT.Copy)
+    ones_and_zeros((3,))
+    for t in range(ROUNDS):
+        qx, qa, lc = "qx%d" % t, "qa%d" % t, "lc%d" % t
+        new = "st%d" % (t + 1)
+        if t == 0:
+            quant("qk", 0, 420, "ktt", 0, 1680)
+        quant("qb", 0, 128, "bt", 0, 512)
+        mm("ps2", 420, "qb", 0, "qk", 0)
+        if t == 0:
+            quant("qe", 0, 512, "ebt", 0, 2048)
+        for b in range(4):
+            mm(ps(4 + b), 512, "qe", 128 * b, qx, 0)
+        for b in range(4):
+            act(("dd", 512 * b, 512 * b + 512), (ps(4 + b), 0, 512), ACT.Copy, scale=0.5)
+        for h in (0, 1):
+            for b in range(4):
+                for gg in range(4):
+                    c = 12 + 16 * (4 * h + gg) + b
+                    vts(("ot", 1040 * h + 4 * gg + b, 1040 * h + 1040, 16), ("kc", 0, 65), ("ps2", c, c + 1), None, OP.is_gt)
+            quant("qo", 260 * h, 260 * h + 260, "ot", 1040 * h, 1040 * h + 1040)
+            if t == 0 and h == 0:
+                for c in range(4):
+                    vcopy(("lt", 512 * c + c, 512 * c + 512, 4), ("upd",))
+                    vcopy(("lt", 2048 + 512 * c + c, 2048 + 512 * c + 512, 4), ("lod",))
+                quant("ql", 0, 512, "lt", 0, 2048)
+                quant("ql", 512, 1024, "lt", 2048, 4096)
+            if h == 0:
+                for c in range(4):
+                    mm(ps(PC0[c]), 256, "ql", 128 * c, "qo", 4, True, False)
+                    mm(ps(PC0[c]), 256, "ql", 512 + 128 * c, "qo", 0, False, True)
+        if t == 0:
+            act(("prt", 0, 512, 4), ("prm",), ACT.Copy, scale=0.0625)
+            act(("prt", 1, 512, 4), ("prm",), ACT.Copy, scale=32.0)
+            act(("prt", 898, 898 + 510, 4), ("prm",), ACT.Copy)
+            act(("prt", 899, 899 + 509, 4), ("prm",), ACT.Copy)
+            for b in range(4):
+                act(("ebt", 512 * b + b, 512 * b + 512, 4), ("krm",), ACT.Copy)
+        act(("tt", 2, 560, 4), ("ps2", 140, 280), ACT.Copy)
+        act(("tt", 3, 560, 4), ("ps2", 280, 420), ACT.Copy)
+        for c in range(4):
+            mm(ps(PC1[c]), 256, "ql", 128 * c, "qo", 264, True, False)
+            mm(ps(PC1[c]), 256, "ql", 512 + 128 * c, "qo", 260, False, True)
+        for c in range(4):
+            for gg in range(4):
+                k = 12 + 16 * gg + c
+                vmax(("rw", k, k + 1), (ps(PC0[c]), gg, 256, 4))
+        for c in range(4):
+            for gg in range(GV - 4, 4):
+                k, z = 76 + 16 * gg + c, 64 * (gg + 4 * (c % 2))
+                act(("sj", z, z + 64), (ps(PC1[c]), gg, 256, 4), ACT.Relu, bias=-1024.0, accum=("rw", k, k + 1))
+            for gg in range(GV - 4):
+                k = 76 + 16 * gg + c
+                vmax(("rw", k, k + 1), (ps(PC1[c]), gg, 256, 4))
+        act(("rv", VR, 140), ("rw", VR, 140), ACT.Identity, bias=-263.5)
+        if t == 0:
+            quant("qp", 0, 448, "prt", 0, 1792)
+        vts(("rv", 0, VR), ("rw", 0, VR), 1287.5, None, OP.subtract)
+        vts(("tt", 0, 560, 4), ("rv",), MAGIC, MAGIC, OP.add, OP.subtract)
+        vtt(("tt", 1, 560, 4), ("rv",), ("tt", 0, 560, 4), OP.subtract)
+        quant("qt", 0, 140, "tt", 0, 560)
+
+        def group_keys():
+            for b in range(4):
+                mm(ps((0, 1, 3, 2)[b]), 128, "qr", 128 * b, "qb", 0)
+            for b in range(4):
+                act(("kf", b, 512, 4), (ps((0, 1, 3, 2)[b]), 0, 128), ACT.Identity, bias=31.5)
+            for c in range(5):
+                act(("ge", 512 * c, 512 * c + 512) if c < 4 else ("is2",), ("kf",), ACT.Sign, bias=("tb", c, c + 1),
+                    accum=("acc", c, c + 1))
+            act(("b5",), ("acc",), ACT.Copy, bias=256.0, scale=-0.5)
+            dma("y", "dk%d" % t, T.kl[8 * t:8 * t + 8, :], T.kf[0:128:16, :], [R("kf")], [])
+
+        if t:
+            group_keys()
+        for q in range(4):
+            mm("ps4", 128, "qt", 12 - 4 * q, "qp", 32 * q, q == 0, q == 3)
+        for q in range(4):
+            mm("ps5", 128, "qt", 12 - 4 * q, "qp", 224 + 32 * q, q == 0, q == 3)
+        if t == 0:
+            quant("qr", 0, 512, "ebt", 0, 2048)
+        vts(("po",), ("ps4", 0, 32), 256.0, None, OP.add)
+        if t == 0:
+            vts(("ia",), ("ip",), 15, None, OP.bitwise_and)
+            vcopy(("icf",), ("ia",))
+            vts(("icb",), ("icf",), -4.0, 0.5, OP.mult, OP.add)
+            vts(("tb",), ("cneg",), ("icb",), None, OP.add)
+            vts(("dum",), ("c16",), ("icf",), None, OP.add)
+            group_keys()
+        vscatter(("lsw",), ("vals",), ("po",))
+        vtrans(("ltr",), ("lsw",))
+        for gg in (0, 1):
+            vtt(("lj", 16 * gg, 16 * gg + 16), ("ltr", 16 * gg, 512, 32), ("ltr", 16 * gg + 1, 512, 32), OP.add)
+        vtrans(("lk",), ("lj",))
+        vcopy(("l16",), ("lk",))
+        for b in (1, 2, 3):
+            act(("sd", 512 * b, 512 * b + 512), ("dd", 512 * b, 512 * b + 512), ACT.Copy, off=("l16",))
+        vgather(("sd", 0, 512), ("dd", 0, 512), ("l16",))
+        msk = "msk%d" % t
+        if t == 0:
+            fill(("neg",), -BIG)
+            fill(("msk0",), BIG)
+            for b in range(4):
+                fill(("sc", 576 * b + 512, 576 * b + 576), 0.0)
+            fill(("at", 256, 512), 0.0)
+        vtt(("em",), ("b5", 1, 5), ("b5", 0, 4), OP.is_equal)
+        vts(("ko",), ("ps5", 0, 32), 31.5, None, OP.add)
+        vtt(("dm",), ("em",), ("dum",), OP.mult)
+        vtt(("mk",), ("b5", 0, 4), ("dm",), OP.max)
+        vtt(("pk",), ("b5", 1, 5), ("dm",), OP.max)
+        vcopy(("mk16",), ("mk",))
+        vts(("pk16",), ("pk",), 1.0, None, OP.subtract)
+        vscatter((msk,), ("neg",), ("mk16",))
+        for b in range(4):
+            vscan(("sc", 576 * b, 576 * b + 512), (msk, 0, 512), ("sd", 512 * b, 512 * b + 512))
+            o, i = ("at", b, 256, 4), ("sc", 576 * b, 576 * b + 576)
+            if b == 2:
+                act(o, i, ACT.Copy, scale=2.0, off=("pk16",))
+            else:
+                vts(o, i, 2.0, None, OP.mult, off=("pk16",))
+        quant(qa, 0, 128, "at", 0, 512)
+        send(t)
+        for b in range(4):
+            mm(ps(b), 128, "qe", 128 * b, qa, 0)
+        for b in range(4):
+            act(("own", 64 * b, 64 * b + 64) if b < 2 else ("in%d" % b, 7, 512, 8), (ps(b), 0, 64), ACT.Copy)
+        if t == 0:
+            for b in range(4):
+                act(("ebt", 512 * b + b, 512 * b + 512, 4), ("idm",), ACT.Copy, scale=0.5)
+            quant("qv", 0, 128, "vs", 0, 512)
+            quant("qh", 0, 512, "ebt", 0, 2048)
+            fill(("msk1",), BIG)
+            fill(("zt", 256, 512), 0.0)
+            fill(("gt", 256, 512), 0.0)
+        wait("t", "ar%d" % t, arrive)
+        for b in (2, 0, 1, 3):
+            mm(ps(4 + b), 448, "qe", 128 * b, lc, 0)
+        for b in (2, 3):
+            for s in range(7):
+                act(("in%d" % b, s, 512, 8), (ps(4 + b), 64 * s, 64 * s + 64), ACT.Copy)
+        for s in range(7):
+            for b in (0, 1):
+                o = ("zt", b, 256, 4) if s == 6 else ("mm", 64 * b, 64 * b + 64)
+                prev = ("own" if s == 0 else "mm", 64 * b, 64 * b + 64)
+                vtt(o, (ps(4 + b), 64 * s, 64 * s + 64), prev, OP.max)
+        for b in (2, 3):
+            vscan(("is%d" % b,), ("m8",), ("in%d" % b,))
+            vcopy(("zt", b, 256, 4), ("is%d" % b, 7, 512, 8))
+        quant("qz", 0, 128, "zt", 0, 512)
+        for b in range(4):
+            mm(ps(b), 128, "qw", 128 * b, "qz", 0)
+        for b in range(4):
+            o, i = ("gt", b, 256, 4), (ps(b), 0, 64)
+            if b % 2:
+                act(o, i, ACT.Relu, scale=0.015625)
+            else:
+                vts(o, i, 0.0, 0.015625, OP.max, OP.mult)
+        quant("qg", 0, 128, "gt", 0, 512)
+        for b in (0, 2, 1, 3):
+            mm(ps(4 + b), 128, "qe", 128 * b, "qg", 0)
+        for b in (0, 2, 1, 3):
+            o, i = ("gb", 64 * b, 64 * b + 64), (ps(4 + b), 0, 64)
+            if b in (0, 1):
+                vts(o, i, 0.5, None, OP.mult)
+            else:
+                act(o, i, ACT.Copy, scale=0.5)
+        for b in (2, 3, 0):
+            mm(ps(b), 512, "qh", 128 * b, qx, 0)
+        for h in (0, 1):
+            mine = (2, 3) if h == 0 else (2, 3, 0)
+            off = ("ko", 16 * h, 16 * h + 16)
+            for b in mine:
+                act(("ge", 1024 * h + 256 * b, 1024 * h + 256 * b + 256), ("gb", 64 * b, 64 * b + 64), ACT.Copy, off=off)
+            for b in [b for b in range(4) if b not in mine] + list(mine):
+                o = (new, 1024 * h + b, 1024 * h + 1024, 4)
+                if b in mine:
+                    vtt(o, (ps(b), 256 * h, 256 * h + 256), ("ge", 1024 * h + 256 * b, 1024 * h + 256 * b + 256), OP.add)
+                else:
+                    vtt(o, ("gb", 64 * b, 64 * b + 64), ("dd", 512 * b + 256 * h, 512 * b + 256 * h + 256), OP.add, off=off)
+            if h == 0:
+                quant("qx%d" % (t + 1), 0, 256, new, 0, 1024)
+        for h in (0, 1):
+            key_half(t + 1, new, h)
+
+    qx = "qx%d" % ROUNDS
+    for k in range(4):
+        dma("y", "ds", T.osc[4 * k:4 * k + 4, :], T[qx + "s"][32 * k:32 * k + 4, :], [R(qx)], [])
+    count["ar0"] = count["ar1"] = arrive
+    for s in SEMAPHORES:
+        if count[s]:
+            wait("q", s, count[s])

@@ -5,7 +5,8 @@ OP, ACT, AX = AluOpType, ActivationFunctionType, AxisListType
 ROUNDS = 2
 BIG = 2.0 ** 60
 MAGIC = 1.5 * 2.0 ** 27
-GV = 5
+GV = 6
+VR = 12 + 16 * GV
 
 SCRATCH = {}
 
@@ -22,14 +23,13 @@ def _codes(names, n):
 
 
 _b("xs st1 st2 ebt dd sd ge", 2048)
-_b("us vs bt at zt gt vals lo lsw ltr sj m8", 512)
-_b("in2 in3 is2 is3", 512)
+_b("us vs bt at zt gt vals lo lsw ltr sj", 512)
 _b("one nul idm krm upd lod prm", 128)
 _b("gw0 gw1 gw2", 8)
 _b("kc", 66)
-_b("ktt", 1680)
+_b("ktt", 1248)
 _b("lt", 4096)
-_b("prt", 1792)
+_b("prt", 1024)
 _b("ot", 2080)
 _b("tt", 560)
 _b("msk0 msk1", 592)
@@ -47,16 +47,15 @@ _b("po ko l16", 32, "uint16")
 _b("mk16 pk16", 4, "uint16")
 _codes("qu qv qb qa0 qa1 qz qg", 128)
 _codes("qx0 qx1 qx2 qw qe qh qr", 512)
-_codes("qk", 420)
-_codes("ql", 1024)
-_codes("qp", 448)
+_codes("qk", 312)
+_codes("ql", 1280)
 _codes("qo", 520)
 _codes("qt", 140)
 _codes("lc0 lc1", 448)
 for _i in range(8):
     SCRATCH["ps%d" % _i] = ("psum", [128, 512], "float32")
 
-SEMAPHORES = ["cv", "cs", "ct", "cq", "ar0", "ar1", "sent",
+SEMAPHORES = ["cv", "cs", "ct", "cq", "ar0", "ar1", "br0", "br1", "sent",
               "dx0", "dx1", "du", "dv", "dwc", "dws", "dlo", "dk0", "dk1", "dy0", "dy1", "do0", "do1", "ds"]
 
 _MASKS = {}
@@ -248,33 +247,33 @@ def rank_program(g, core, T, topo):
     dma("y", "dws", T.qws[:, 0:512], T.ws[:, 0:512], [], [R("qws")])
     dma("y", "dv", T.vs[:, 0:512], T.v[:, 0:512], [], [R("vs")])
 
-    for n in ("gw0", "gw1", "gw2"):
-        fill((n,), 0.0)
     fill(("one",), 1.0)
+    fill(("gw0",), 0.0)
     fill(("nul",), 0.0)
-    fill(("ktt",), 0.0)
-    fill(("krm",), 0.0)
     fill(("ebt",), 0.0)
-    fill(("prt",), 0.0)
+    fill(("ktt",), 0.0)
+    sel(("idm",), ("one",), [[-1, 128]], OP.is_equal, 0.0, 0, 1)
     for i in range(6):
         sel(("gw0",), ("gw0",), [[-16, 8]], OP.not_equal, 2.0 ** (i - 1), -i, 1)
-    for i in range(6):
-        w = "gw1" if i < 2 else "gw2"
-        sel((w,), (w,), [[-16, 8]], OP.not_equal, 8.0 * 2 ** i if i < 2 else 0.125 * 2 ** i, -i, 1)
-    sel(("idm",), ("one",), [[-1, 128]], OP.is_equal, 0.0, 0, 1)
-    iota(("kc", 0, 65), [[1, 65]], -32, 0)
+    sel(("gw1",), ("gw0",), [[16, 8]], OP.is_ge, 0.0, 1, -1)
+    sel(("gw2",), ("gw0",), [[-16, 8]], OP.is_ge, 0.0, -2, 1)
     sel(("upd",), ("one",), [[1, 128]], OP.is_gt, 0.0, 0, -1)
     sel(("upd",), ("upd",), [[1, 128]], OP.not_equal, 1024.0, 0, -1)
     sel(("lod",), ("one",), [[-1, 128]], OP.is_gt, 0.0, 0, 1)
     sel(("lod",), ("lod",), [[-1, 128]], OP.not_equal, -1024.0, 0, 1)
+    iota(("kc", 0, 65), [[1, 65]], -32, 0)
     sel(("prm",), ("one",), [[-1, 4], [-4, 32]], OP.is_equal, 0.0, 0, 1)
     for i in range(6):
-        sel(("krm",), ("krm",), [[-16, 8], [0, 16]], OP.not_equal, 2.0 ** (i - 1), -i, 1)
+        sel(("krm",), ("krm" if i else "nul",), [[-16, 8], [0, 16]], OP.not_equal, 2.0 ** (i - 1), -i, 1)
     iota(("ip",), [[0, 1]], 0, 1)
     iota(("cneg",), [[-1, 5]], 0, 0)
     iota(("c16",), [[16, 4]], 513, 0)
     iota(("lo",), [[0, 2], [1, 256]], 0, 0)
     iota(("vals",), [[256, 2], [0, 256]], 0, 0)
+    for b in range(4):
+        iota(("sc", 576 * b + 512, 576 * b + 576), [[0, 64]], 0, 0)
+    for n in ("at", "zt", "gt"):
+        iota((n, 256, 512), [[0, 256]], 0, 0)
     dma("y", "dlo", T.vals[1:128:16, :], T.lo[1:128:16, :], [R("lo")], [R("vals")])
 
     def ones_and_zeros(cs):
@@ -285,48 +284,53 @@ def rank_program(g, core, T, topo):
                         act(("lt", 2048 * s + 512 * c + b, 2048 * s + 512 * c + 512, 4), ("one" if o else "nul",), ACT.Copy)
     ones_and_zeros((0, 1, 2))
     for b in range(4):
-        for k in range(3):
-            act(("ktt", 560 * k + 48 + 5 * b, 560 * k + 560, 64), ("gw%d" % k,), ACT.Copy)
+        act(("ktt", 5 * b, 128, 16), ("gw0",), ACT.Copy)
+        act(("ktt", 128 + 48 + 5 * b, 688, 64), ("gw1",), ACT.Copy, scale=16.0)
+        act(("ktt", 688 + 48 + 5 * b, 1248, 64), ("gw2",), ACT.Copy, scale=0.25)
+    fill(("prt",), 0.0)
+    fill(("rw", 0, VR), 1287.5)
+    fill(("rw", VR, 140), 263.5)
     quant("qu", 0, 128, "us", 0, 512)
-    fill(("rw", 0, 12 + 16 * GV), 1287.5)
-    fill(("rw", 12 + 16 * GV, 140), 263.5)
-    fill(("m8",), BIG)
-    fill(("m8", 0, 512, 8), -BIG)
+    for b in range(4):
+        vcopy(("ebt", 512 * b + b, 512 * b + 512, 4), ("idm",))
+    quant("qe", 0, 512, "ebt", 0, 2048)
+    fill(("neg",), -BIG)
 
-    others = [r for r in range(N) if r != rank]
-    near = [r for r in others if topo.chip(T.cores[r]) == topo.chip(core)]
-    far = [r for r in others if r not in near]
-    fmask = topo.mask(core, T.cores[far[0]])
-    nmask = topo.mask(core, T.cores[near[0]]) & ~fmask
-    arrive = 0
-    for r in others:
-        arrive += 2 * bin(nmask if r in near else fmask).count("1")
+    lots = ((1, 2, 4, 6), (3, 5, 7))
+    near = [x for x in range(1, N) if topo.chip(T.cores[rank ^ x]) == topo.chip(core)]
+    far = [x for x in range(1, N) if x not in near]
+    fmask = topo.mask(core, T.cores[rank ^ far[0]])
+    nmask = topo.mask(core, T.cores[rank ^ near[0]]) & ~fmask
+
+    def arrive(lot):
+        return sum(2 * bin(nmask if x in near else fmask).count("1") for x in lots[lot])
 
     def send(t):
         qa, lc = "qa%d" % t, "lc%d" % t
         n = need("q", [R(qa)], [])
         for s in n:
             wait("q", s, n[s])
-        for plane in (0, 1):
-            ts = []
-            for group, m in ((far, fmask), (near, nmask)):
-                ids, dsts = [], []
-                for r in group:
-                    rid, pid = topo.addr(T.cores[r])[:2]
-                    slot = rank - (1 if rank > r else 0)
-                    ids.append(DstId(rid=rid, pnc=pid))
-                    dsts.append(T[lc + "s"][:, 64 * slot:64 * slot + 64] if plane
-                                else T[lc][:, 64 * slot:64 * slot + 64].bitcast(dt.uint8))
-                src = T[qa + "s"][:, 0:64] if plane else T[qa][:, 0:64].bitcast(dt.uint8)
-                ts.append(RemoteDMATransfer(dst_ids=ids, dma_engine_mask=m, remote_sem=T.sem["ar%d" % t],
-                                            srcs=[src], dsts=dsts))
-                count["sent"] += bin(m).count("1")
-            g.remote_dma_fused(ts, local_sem=T.sem.sent)
+        for lot in (0, 1):
+            for plane in (0, 1):
+                ts = []
+                for group, m in ((far, fmask), (near, nmask)):
+                    ids, dsts = [], []
+                    for x in lots[lot]:
+                        if x in group:
+                            rid, pid = topo.addr(T.cores[rank ^ x])[:2]
+                            c = 256 * lot + 64 * lots[lot].index(x)
+                            ids.append(DstId(rid=rid, pnc=pid))
+                            dsts.append(T[lc + "s"][:, c:c + 64] if plane else T[lc][:, c:c + 64].bitcast(dt.uint8))
+                    if ids:
+                        src = T[qa + "s"][:, 0:64] if plane else T[qa][:, 0:64].bitcast(dt.uint8)
+                        ts.append(RemoteDMATransfer(dst_ids=ids, dma_engine_mask=m, remote_sem=T.sem["%sr%d" % ("ab"[lot], t)],
+                                                    srcs=[src], dsts=dsts))
+                        count["sent"] += bin(m).count("1")
+                g.remote_dma_fused(ts, local_sem=T.sem.sent)
 
     def ps(i):
         return "ps%d" % i
-    PC0, PC1 = [4, 5, 6, 7], [0, 1, 3, 2]
-    VR = 12 + 16 * GV
+    PC0, PC1, HB = [4, 5, 6, 7], [0, 1, 3, 2], {2: 4, 3: 5, 0: 6}
 
     def key_half(t, state, h):
         qx = "qx%d" % t
@@ -345,50 +349,48 @@ def rank_program(g, core, T, topo):
 
     key_half(0, "xs", 0)
     key_half(0, "xs", 1)
-    for b in range(4):
-        act(("ebt", 512 * b + b, 512 * b + 512, 4), ("idm",), ACT.Copy)
     ones_and_zeros((3,))
+    for c in range(4):
+        vcopy(("lt", 512 * c + c, 512 * c + 512, 4), ("upd",))
+        vcopy(("lt", 2048 + 512 * c + c, 2048 + 512 * c + 512, 4), ("lod",))
     for t in range(ROUNDS):
         qx, qa, lc = "qx%d" % t, "qa%d" % t, "lc%d" % t
         new = "st%d" % (t + 1)
         if t == 0:
-            quant("qk", 0, 420, "ktt", 0, 1680)
+            quant("qk", 0, 312, "ktt", 0, 1248)
+        mm(ps(4), 512, "qe", 0, qx, 0)
         quant("qb", 0, 128, "bt", 0, 512)
-        mm("ps2", 420, "qb", 0, "qk", 0)
-        if t == 0:
-            quant("qe", 0, 512, "ebt", 0, 2048)
-        for b in range(4):
+        mm("ps2", 312, "qb", 0, "qk", 0)
+        for b in (1, 2, 3):
             mm(ps(4 + b), 512, "qe", 128 * b, qx, 0)
-        for b in range(4):
+        if t == 0:
+            fill(("msk0",), BIG)
+        vts(("dd", 0, 512), (ps(4), 0, 512), 0.5, None, OP.mult)
+        for b in (1, 2, 3):
             act(("dd", 512 * b, 512 * b + 512), (ps(4 + b), 0, 512), ACT.Copy, scale=0.5)
+        if t == 0:
+            quant("ql", 256, 768, "lt", 0, 2048)
+            quant("ql", 768, 1280, "lt", 2048, 4096)
         for h in (0, 1):
             for b in range(4):
                 for gg in range(4):
-                    c = 12 + 16 * (4 * h + gg) + b
+                    c = 4 * (4 * h + gg) + b
                     vts(("ot", 1040 * h + 4 * gg + b, 1040 * h + 1040, 16), ("kc", 0, 65), ("ps2", c, c + 1), None, OP.is_gt)
             quant("qo", 260 * h, 260 * h + 260, "ot", 1040 * h, 1040 * h + 1040)
-            if t == 0 and h == 0:
-                for c in range(4):
-                    vcopy(("lt", 512 * c + c, 512 * c + 512, 4), ("upd",))
-                    vcopy(("lt", 2048 + 512 * c + c, 2048 + 512 * c + 512, 4), ("lod",))
-                quant("ql", 0, 512, "lt", 0, 2048)
-                quant("ql", 512, 1024, "lt", 2048, 4096)
             if h == 0:
                 for c in range(4):
-                    mm(ps(PC0[c]), 256, "ql", 128 * c, "qo", 4, True, False)
-                    mm(ps(PC0[c]), 256, "ql", 512 + 128 * c, "qo", 0, False, True)
+                    mm(ps(PC0[c]), 256, "ql", 256 + 128 * c, "qo", 4, True, False)
+                    mm(ps(PC0[c]), 256, "ql", 768 + 128 * c, "qo", 0, False, True)
         if t == 0:
             act(("prt", 0, 512, 4), ("prm",), ACT.Copy, scale=0.0625)
             act(("prt", 1, 512, 4), ("prm",), ACT.Copy, scale=32.0)
-            act(("prt", 898, 898 + 510, 4), ("prm",), ACT.Copy)
-            act(("prt", 899, 899 + 509, 4), ("prm",), ACT.Copy)
-            for b in range(4):
-                act(("ebt", 512 * b + b, 512 * b + 512, 4), ("krm",), ACT.Copy)
-        act(("tt", 2, 560, 4), ("ps2", 140, 280), ACT.Copy)
-        act(("tt", 3, 560, 4), ("ps2", 280, 420), ACT.Copy)
+            act(("prt", 514, 1024, 4), ("prm",), ACT.Copy)
+            act(("prt", 515, 1024, 4), ("prm",), ACT.Copy)
+        act(("tt", 2, 560, 4), ("ps2", 32, 172), ACT.Copy)
+        act(("tt", 3, 560, 4), ("ps2", 172, 312), ACT.Copy)
         for c in range(4):
-            mm(ps(PC1[c]), 256, "ql", 128 * c, "qo", 264, True, False)
-            mm(ps(PC1[c]), 256, "ql", 512 + 128 * c, "qo", 260, False, True)
+            mm(ps(PC1[c]), 256, "ql", 256 + 128 * c, "qo", 264, True, False)
+            mm(ps(PC1[c]), 256, "ql", 768 + 128 * c, "qo", 260, False, True)
         for c in range(4):
             for gg in range(4):
                 k = 12 + 16 * gg + c
@@ -401,9 +403,9 @@ def rank_program(g, core, T, topo):
                 k = 76 + 16 * gg + c
                 vmax(("rw", k, k + 1), (ps(PC1[c]), gg, 256, 4))
         act(("rv", VR, 140), ("rw", VR, 140), ACT.Identity, bias=-263.5)
-        if t == 0:
-            quant("qp", 0, 448, "prt", 0, 1792)
         vts(("rv", 0, VR), ("rw", 0, VR), 1287.5, None, OP.subtract)
+        if t == 0:
+            quant("ql", 0, 256, "prt", 0, 1024)
         vts(("tt", 0, 560, 4), ("rv",), MAGIC, MAGIC, OP.add, OP.subtract)
         vtt(("tt", 1, 560, 4), ("rv",), ("tt", 0, 560, 4), OP.subtract)
         quant("qt", 0, 140, "tt", 0, 560)
@@ -414,7 +416,7 @@ def rank_program(g, core, T, topo):
             for b in range(4):
                 act(("kf", b, 512, 4), (ps((0, 1, 3, 2)[b]), 0, 128), ACT.Identity, bias=31.5)
             for c in range(5):
-                act(("ge", 512 * c, 512 * c + 512) if c < 4 else ("is2",), ("kf",), ACT.Sign, bias=("tb", c, c + 1),
+                act(("ge", 512 * c, 512 * c + 512) if c < 4 else ("sj",), ("kf",), ACT.Sign, bias=("tb", c, c + 1),
                     accum=("acc", c, c + 1))
             act(("b5",), ("acc",), ACT.Copy, bias=256.0, scale=-0.5)
             dma("y", "dk%d" % t, T.kl[8 * t:8 * t + 8, :], T.kf[0:128:16, :], [R("kf")], [])
@@ -422,10 +424,12 @@ def rank_program(g, core, T, topo):
         if t:
             group_keys()
         for q in range(4):
-            mm("ps4", 128, "qt", 12 - 4 * q, "qp", 32 * q, q == 0, q == 3)
+            mm("ps4", 128, "qt", 12 - 4 * q, "ql", 32 * q, q == 0, q == 3)
         for q in range(4):
-            mm("ps5", 128, "qt", 12 - 4 * q, "qp", 224 + 32 * q, q == 0, q == 3)
+            mm("ps5", 128, "qt", 12 - 4 * q, "ql", 128 + 32 * q, q == 0, q == 3)
         if t == 0:
+            for b in range(4):
+                act(("ebt", 512 * b + b, 512 * b + 512, 4), ("krm",), ACT.Copy)
             quant("qr", 0, 512, "ebt", 0, 2048)
         vts(("po",), ("ps4", 0, 32), 256.0, None, OP.add)
         if t == 0:
@@ -445,12 +449,6 @@ def rank_program(g, core, T, topo):
             act(("sd", 512 * b, 512 * b + 512), ("dd", 512 * b, 512 * b + 512), ACT.Copy, off=("l16",))
         vgather(("sd", 0, 512), ("dd", 0, 512), ("l16",))
         msk = "msk%d" % t
-        if t == 0:
-            fill(("neg",), -BIG)
-            fill(("msk0",), BIG)
-            for b in range(4):
-                fill(("sc", 576 * b + 512, 576 * b + 576), 0.0)
-            fill(("at", 256, 512), 0.0)
         vtt(("em",), ("b5", 1, 5), ("b5", 0, 4), OP.is_equal)
         vts(("ko",), ("ps5", 0, 32), 31.5, None, OP.add)
         vtt(("dm",), ("em",), ("dum",), OP.mult)
@@ -462,7 +460,7 @@ def rank_program(g, core, T, topo):
         for b in range(4):
             vscan(("sc", 576 * b, 576 * b + 512), (msk, 0, 512), ("sd", 512 * b, 512 * b + 512))
             o, i = ("at", b, 256, 4), ("sc", 576 * b, 576 * b + 576)
-            if b == 2:
+            if b in (1, 2):
                 act(o, i, ACT.Copy, scale=2.0, off=("pk16",))
             else:
                 vts(o, i, 2.0, None, OP.mult, off=("pk16",))
@@ -471,29 +469,29 @@ def rank_program(g, core, T, topo):
         for b in range(4):
             mm(ps(b), 128, "qe", 128 * b, qa, 0)
         for b in range(4):
-            act(("own", 64 * b, 64 * b + 64) if b < 2 else ("in%d" % b, 7, 512, 8), (ps(b), 0, 64), ACT.Copy)
+            act(("own", 64 * b, 64 * b + 64), (ps(b), 0, 64), ACT.Copy)
         if t == 0:
             for b in range(4):
                 act(("ebt", 512 * b + b, 512 * b + 512, 4), ("idm",), ACT.Copy, scale=0.5)
             quant("qv", 0, 128, "vs", 0, 512)
             quant("qh", 0, 512, "ebt", 0, 2048)
             fill(("msk1",), BIG)
-            fill(("zt", 256, 512), 0.0)
-            fill(("gt", 256, 512), 0.0)
-        wait("t", "ar%d" % t, arrive)
-        for b in (2, 0, 1, 3):
-            mm(ps(4 + b), 448, "qe", 128 * b, lc, 0)
-        for b in (2, 3):
-            for s in range(7):
-                act(("in%d" % b, s, 512, 8), (ps(4 + b), 64 * s, 64 * s + 64), ACT.Copy)
-        for s in range(7):
-            for b in (0, 1):
-                o = ("zt", b, 256, 4) if s == 6 else ("mm", 64 * b, 64 * b + 64)
-                prev = ("own" if s == 0 else "mm", 64 * b, 64 * b + 64)
-                vtt(o, (ps(4 + b), 64 * s, 64 * s + 64), prev, OP.max)
-        for b in (2, 3):
-            vscan(("is%d" % b,), ("m8",), ("in%d" % b,))
-            vcopy(("zt", b, 256, 4), ("is%d" % b, 7, 512, 8))
+        wait("t", "ar%d" % t, arrive(0))
+        for b in range(4):
+            mm(ps(4 + b), 256, "qe", 128 * b, lc, 0)
+        for s in range(4):
+            for b in range(4):
+                o, w = ("mm", 64 * b, 64 * b + 64), ("own" if s == 0 else "mm", 64 * b, 64 * b + 64)
+                vtt(o, (ps(4 + b), 64 * s, 64 * s + 64), w, OP.max)
+        for b in (2, 3, 0):
+            mm(ps(HB[b]), 512, "qh", 128 * b, qx, 0)
+        wait("t", "br%d" % t, arrive(1))
+        for b in range(4):
+            mm(ps(b), 192, "qe", 128 * b, lc, 256)
+        for s in range(3):
+            for b in range(4):
+                w = ("mm", 64 * b, 64 * b + 64)
+                vtt(("zt", b, 256, 4) if s == 2 else w, (ps(b), 64 * s, 64 * s + 64), w, OP.max)
         quant("qz", 0, 128, "zt", 0, 512)
         for b in range(4):
             mm(ps(b), 128, "qw", 128 * b, "qz", 0)
@@ -505,15 +503,13 @@ def rank_program(g, core, T, topo):
                 vts(o, i, 0.0, 0.015625, OP.max, OP.mult)
         quant("qg", 0, 128, "gt", 0, 512)
         for b in (0, 2, 1, 3):
-            mm(ps(4 + b), 128, "qe", 128 * b, "qg", 0)
+            mm(ps(b), 128, "qe", 128 * b, "qg", 0)
         for b in (0, 2, 1, 3):
-            o, i = ("gb", 64 * b, 64 * b + 64), (ps(4 + b), 0, 64)
+            o, i = ("gb", 64 * b, 64 * b + 64), (ps(b), 0, 64)
             if b in (0, 1):
                 vts(o, i, 0.5, None, OP.mult)
             else:
                 act(o, i, ACT.Copy, scale=0.5)
-        for b in (2, 3, 0):
-            mm(ps(b), 512, "qh", 128 * b, qx, 0)
         for h in (0, 1):
             mine = (2, 3) if h == 0 else (2, 3, 0)
             off = ("ko", 16 * h, 16 * h + 16)
@@ -522,7 +518,7 @@ def rank_program(g, core, T, topo):
             for b in [b for b in range(4) if b not in mine] + list(mine):
                 o = (new, 1024 * h + b, 1024 * h + 1024, 4)
                 if b in mine:
-                    vtt(o, (ps(b), 256 * h, 256 * h + 256), ("ge", 1024 * h + 256 * b, 1024 * h + 256 * b + 256), OP.add)
+                    vtt(o, (ps(HB[b]), 256 * h, 256 * h + 256), ("ge", 1024 * h + 256 * b, 1024 * h + 256 * b + 256), OP.add)
                 else:
                     vtt(o, ("gb", 64 * b, 64 * b + 64), ("dd", 512 * b + 256 * h, 512 * b + 256 * h + 256), OP.add, off=off)
             if h == 0:
@@ -533,7 +529,8 @@ def rank_program(g, core, T, topo):
     qx = "qx%d" % ROUNDS
     for k in range(4):
         dma("y", "ds", T.osc[4 * k:4 * k + 4, :], T[qx + "s"][32 * k:32 * k + 4, :], [R(qx)], [])
-    count["ar0"] = count["ar1"] = arrive
+    count["ar0"] = count["ar1"] = arrive(0)
+    count["br0"] = count["br1"] = arrive(1)
     for s in SEMAPHORES:
         if count[s]:
             wait("q", s, count[s])

@@ -4,9 +4,11 @@ from concourse.mybir import dt, AluOpType, AxisListType, ActivationFunctionType
 OP, ACT, AX = AluOpType, ActivationFunctionType, AxisListType
 ROUNDS = 2
 BIG = 2.0 ** 60
-MAGIC = 1.5 * 2.0 ** 27
-GV = 6
-VR = 12 + 16 * GV
+M16 = 3072.0
+TRIES = 24
+VR = 108
+RW = 1032.0
+RS = 520.0
 
 SCRATCH = {}
 
@@ -22,9 +24,10 @@ def _codes(names, n):
         SCRATCH[name + "s"] = ("sbuf", [128, n], "uint8")
 
 
-_b("xs st1 st2 ebt dd sd ge", 2048)
+_b("xs st1 st2 ebt ebk dd sd ge", 2048)
 _b("us vs bt at zt gt vals lo lsw ltr sj", 512)
-_b("one nul idm krm upd lod prm", 128)
+_b("jk", 2560)
+_b("one nul idm blk upd lod prm", 128)
 _b("gw0 gw1 gw2", 8)
 _b("kc", 66)
 _b("ktt", 1248)
@@ -36,12 +39,14 @@ _b("msk0 msk1", 592)
 _b("sc", 2304)
 _b("neg", 64)
 _b("own mm gb", 256)
+_b("hi", 140)
 _b("rw rv", 140, "float32")
 _b("kf yb", 512, "float32")
 _b("lj lk", 32, "float32")
+_b("kng", 8, "float32")
 _b("acc b5 cneg tb", 5, "float32")
 _b("em dm mk pk dum c16", 4, "float32")
-_b("icf icb", 1, "float32")
+_b("icf icb wcl", 1, "float32")
 _b("ip ia", 1, "int32")
 _b("po ko l16", 32, "uint16")
 _b("mk16 pk16", 4, "uint16")
@@ -56,9 +61,10 @@ for _i in range(8):
     SCRATCH["ps%d" % _i] = ("psum", [128, 512], "float32")
 
 SEMAPHORES = ["cv", "cs", "ct", "cq", "ar0", "ar1", "br0", "br1", "sent",
-              "dx0", "dx1", "du", "dv", "dwc", "dws", "dlo", "dk0", "dk1", "dy0", "dy1", "do0", "do1", "ds"]
+              "dx0", "dx1", "du", "dv", "dwc", "dws", "dlo", "dz0", "dz1", "dk0", "dk1", "dy0", "dy1", "do0", "do1", "ds"]
 
 _MASKS = {}
+_PLAN = []
 
 
 def _cols(a, b, st):
@@ -68,6 +74,101 @@ def _cols(a, b, st):
             m |= 1 << i
         _MASKS[(a, b, st)] = m
     return _MASKS[(a, b, st)]
+
+
+def plan(ops, tries):
+    wr, rd, pred = {}, {}, []
+    for i, o in enumerate(ops):
+        p = set()
+        for name, m in o["reads"]:
+            for wm, j in wr.get(name, []):
+                if wm & m:
+                    p.add(j)
+            if name[:2] == "ps":
+                for rm, j in rd.get(name, []):
+                    if ops[j]["e"] != o["e"]:
+                        p.add(j)
+        for name, m in o["writes"]:
+            for om, j in wr.get(name, []) + rd.get(name, []):
+                if om & m:
+                    p.add(j)
+        p.discard(i)
+        for name, m in o["writes"]:
+            wr[name] = [w for w in wr.get(name, []) if w[0] & ~m] + [(m, i)]
+            rd[name] = [r for r in rd.get(name, []) if r[0] & ~m]
+        for name, m in o["reads"]:
+            rd[name] = rd.get(name, []) + [(m, i)]
+        pred.append(sorted(p))
+    n = len(ops)
+    every = range(n)
+    succ = [[] for _ in ops]
+    for i in every:
+        for j in pred[i]:
+            succ[j].append(i)
+    eng = [o["e"] for o in ops]
+    hold = [o["hold"] for o in ops]
+    lat = [o["lat"] for o in ops]
+    WAKE = 0.18
+
+    def free_of(j, i):
+        return eng[j] == "t" and eng[i] == "t" or eng[i] == "n"
+
+    def gap(j, i):
+        return lat[j] if free_of(j, i) else lat[j] + WAKE
+
+    def place(order, early):
+        t = [0.0] * n
+        busy = {e: [] for e in eng}
+        for i in order:
+            d = hold[i]
+            if early:
+                lo = max([0.0] + [t[j] + gap(j, i) for j in pred[i]])
+            else:
+                lo = max([lat[i]] + [t[k] + gap(i, k) for k in succ[i]]) - d
+            if eng[i] != "n":
+                b = busy[eng[i]]
+                z = len(b)
+                while z and b[z - 1][1] > lo + 1e-9:
+                    z -= 1
+                while z < len(b) and b[z][0] < lo + d - 1e-9:
+                    lo = max(lo, b[z][1])
+                    z += 1
+                b.insert(z, (lo, lo + d))
+            t[i] = lo if early else lo + d
+        return t
+
+    def run(order, tensor, wake, others):
+        t = [0.0] * n
+        free = {}
+        end = 0.0
+        for i in order:
+            s = free.get(eng[i], 0.0)
+            for j in pred[i]:
+                x = t[j] if free_of(j, i) else t[j] + wake
+                if x > s:
+                    s = x
+            f = tensor if eng[i] == "t" else others if eng[i] == "n" else 1.0
+            if eng[i] != "n":
+                free[eng[i]] = s + hold[i] * f
+            t[i] = s + lat[i] * f
+            end = max(end, t[i])
+        return end
+    best, seed = None, 1
+    for k in range(tries):
+        way = [0.0] * n
+        for i in range(n - 1, -1, -1):
+            seed = (seed * 1103515245 + 12345) % 2147483648
+            w = lat[i] * (1.0 + (0.8 * seed / 2147483648 - 0.4 if k else 0.0))
+            way[i] = max([w] + [w + gap(i, x) - lat[i] + way[x] for x in succ[i]])
+        t = place(sorted(every, key=lambda i: (-way[i], i)), True)
+        for _ in range(3):
+            order = sorted(every, key=lambda i: (t[i], i))
+            score = sum(run(order, *v) for v in ((1.0, 0.1, 1.0), (1.0, 0.18, 1.3), (2.0, 0.18, 1.0), (1.0, 0.25, 0.8)))
+            if best is None or score < best[0]:
+                best = (score, order)
+            late = place(sorted(every, key=lambda i: (-(t[i] + lat[i]), -i)), False)
+            t = place(sorted(every, key=lambda i: (-late[i], i)), True)
+    return best[1]
 
 
 def prog(g, T):
@@ -115,17 +216,27 @@ def prog(g, T):
             rd[name] = [r for r in rd.get(name, [])
                         if not (r[2] == e and e != "dma" and r[0] & ~m == 0)] + [(m, tok, e)]
 
-    def emit(e, call, reads, writes, sem=None):
+    def issue(o):
+        e = o["e"]
+        if e == "n":
+            return
+        reads = [r for r in o["reads"] if r[0][0] != "@"]
+        writes = [w for w in o["writes"] if w[0][0] != "@"]
+        for s, v in o["pre"]:
+            wait(e, s, v)
         n = need(e, reads, writes)
         for s in sorted(n, key=lambda s: -n[s]):
             wait(e, s, n[s])
-        s = sem or csem[e]
-        k = 16 if sem else 1
-        call().then_inc(T.sem[s], k)
+        if o["sem"] == "sent":
+            o["call"]()
+            return
+        s = o["sem"] or csem[e]
+        k = 16 if o["sem"] else 1
+        o["call"]().then_inc(T.sem[s], k)
         count[s] += k
         snap[(s, count[s])] = dict(known[e])
-        note("dma" if sem else e, reads, writes, (s, count[s]))
-    return eng, count, wait, emit, need
+        note("dma" if o["sem"] else e, reads, writes, (s, count[s]))
+    return eng, count, wait, issue
 
 
 def rank_program(g, core, T, topo):
@@ -133,8 +244,14 @@ def rank_program(g, core, T, topo):
     if rank is None:
         return
     N = len(T.cores)
-    eng, count, wait, emit, need = prog(g, T)
+    eng, count, wait, issue = prog(g, T)
     V, S, PE = g.vector, g.scalar, g.tensor
+    ops = []
+    CYC = 0.00083
+
+    def emit(e, call, reads, writes, cost, sem=None, lat=None, pre=()):
+        ops.append({"e": e, "call": call, "reads": reads, "writes": writes, "sem": sem, "pre": list(pre),
+                    "hold": cost, "lat": cost if lat is None else lat})
 
     def R(name, a=0, b=None, st=1):
         if name[:2] == "ps":
@@ -148,13 +265,20 @@ def rank_program(g, core, T, topo):
     def both(x):
         return A(*x), R(*x)
 
+    def size(x):
+        return len(range(x[1] if len(x) > 1 else 0, x[2] if len(x) > 2 else SCRATCH[x[0]][1][1], x[3] if len(x) > 3 else 1))
+
+    def vcost(*xs, half=True):
+        short = all(SCRATCH[x[0]][2] in ("bfloat16", "uint16") for x in xs)
+        return 0.05 + CYC * max(64, max(size(x) for x in xs) * (0.5 if short and half else 1.0))
+
     def fill(x, c):
         a, r = both(x)
-        emit("v", lambda: V.memset(a, c), [], [r])
+        emit("v", lambda: V.memset(a, c), [], [r], vcost(x))
 
     def vcopy(o, i):
         (oa, orr), (ia, ir) = both(o), both(i)
-        emit("v", lambda: V.tensor_copy(oa, ia), [ir], [orr])
+        emit("v", lambda: V.tensor_copy(oa, ia), [ir], [orr], vcost(o, i))
 
     def vts(o, i, s1, s2, op0, op1=None, off=None):
         (oa, orr), (ia, ir) = both(o), both(i)
@@ -162,97 +286,113 @@ def rank_program(g, core, T, topo):
         if isinstance(s1, tuple):
             s1, r1 = both(s1)
             rs.append(r1)
+        cost = vcost(o, i)
         if off:
             fa, fr = both(off)
             ia = ia.indirect(fa)
             rs.append(fr)
+            cost = 0.05 + 1.5 * CYC * size(o)
         if op1 is None:
-            emit("v", lambda: V.tensor_scalar(oa, ia, s1, None, op0), rs, [orr])
+            emit("v", lambda: V.tensor_scalar(oa, ia, s1, None, op0), rs, [orr], cost)
         else:
-            emit("v", lambda: V.tensor_scalar(oa, ia, s1, s2, op0, op1), rs, [orr])
+            emit("v", lambda: V.tensor_scalar(oa, ia, s1, s2, op0, op1), rs, [orr], cost)
 
     def vtt(o, i0, i1, op, off=None):
         (oa, orr), (a0, r0), (a1, r1) = both(o), both(i0), both(i1)
         rs = [r0, r1]
+        cost = vcost(o, i1, half=False)
         if off:
             fa, fr = both(off)
             a0 = a0.indirect(fa)
             rs.append(fr)
-        emit("v", lambda: V.tensor_tensor(oa, a0, a1, op), rs, [orr])
+            cost = 0.05 + 1.5 * CYC * size(o)
+        emit("v", lambda: V.tensor_tensor(oa, a0, a1, op), rs, [orr], cost)
 
     def vscan(o, mask, data):
         (oa, orr), (ma, mr), (da, dr) = both(o), both(mask), both(data)
-        emit("v", lambda: V.tensor_tensor_scan(oa, ma, da, -BIG, OP.min, OP.max), [mr, dr], [orr])
+        emit("v", lambda: V.tensor_tensor_scan(oa, ma, da, -BIG, OP.min, OP.max), [mr, dr], [orr], vcost(o, data))
 
     def vgather(o, i, off):
         (oa, orr), (ia, ir), (fa, fr) = both(o), both(i), both(off)
-        emit("v", lambda: V.tensor_copy(oa, ia.indirect(fa)), [ir, fr], [orr])
+        emit("v", lambda: V.tensor_copy(oa, ia.indirect(fa)), [ir, fr], [orr], 0.05 + 1.5 * CYC * size(o))
 
     def vscatter(o, i, off):
         (oa, orr), (ia, ir), (fa, fr) = both(o), both(i), both(off)
-        emit("v", lambda: V.tensor_copy(oa.indirect(fa), ia), [ir, fr], [orr])
+        emit("v", lambda: V.tensor_copy(oa.indirect(fa), ia), [ir, fr], [orr], 0.05 + 3.0 * CYC * size(i))
 
     def vtrans(o, i):
         (oa, orr), (ia, ir) = both(o), both(i)
-        emit("v", lambda: V.transpose(oa, ia), [ir], [orr])
+        emit("v", lambda: V.transpose(oa, ia), [ir], [orr], vcost(o, i))
 
-    def vmax(o, i):
+    def vreduce(o, i, op):
         (oa, orr), (ia, ir) = both(o), both(i)
-        emit("v", lambda: V.tensor_reduce(oa, ia, AX.X, OP.max), [ir], [orr])
+        emit("v", lambda: V.tensor_reduce(oa, ia, AX.X, op), [ir], [orr], vcost(i, half=False))
 
     def quant(q, a, b, x, xa, xb):
         emit("v", lambda: V.quantize_mx(T[q][:, a:b], T[q + "s"][:, a:b], T[x][:, xa:xb]),
-             [R(x, xa, xb)], [R(q, a, b)])
+             [R(x, xa, xb)], [R(q, a, b)], 0.012 + 0.00022 * (xb - xa))
 
-    def act(o, i, f, bias=0.0, scale=1.0, off=None, accum=None):
+    def act(o, i, f, bias=0.0, scale=1.0, off=None, accum=None, lat=None):
         (oa, orr), (ia, ir) = both(o), both(i)
         rs, ws = [ir], [orr]
         if isinstance(bias, tuple):
             bias, r1 = both(bias)
             rs.append(r1)
+        if isinstance(scale, tuple):
+            scale, r1 = both(scale)
+            rs.append(r1)
+        cost = 0.065 + CYC * size(o)
         if off:
             fa, fr = both(off)
             ia = ia.indirect(fa)
             rs.append(fr)
+            cost = 0.065 + 1.5 * CYC * size(o)
         if accum:
             aa, ar = both(accum)
             ws.append(ar)
-            emit("s", lambda: S.activation(oa, ia, f, bias=bias, scale=scale, accum_out=aa), rs, ws)
+            emit("s", lambda: S.activation(oa, ia, f, bias=bias, scale=scale, accum_out=aa), rs, ws, cost + 0.02)
         else:
-            emit("s", lambda: S.activation(oa, ia, f, bias=bias, scale=scale), rs, ws)
+            emit("s", lambda: S.activation(oa, ia, f, bias=bias, scale=scale), rs, ws, cost, lat=lat)
 
-    def mm(ps, n, w, wa, x, xa, start=True, stop=True):
+    def mm(ps, n, w, wa, x, xa, start=True, stop=True, pre=()):
         emit("t", lambda: PE.matmul_mx(T[ps][:, 0:n], T[w][:, wa:wa + 128], T[w + "s"][:, wa:wa + 128],
                                        T[x][:, xa:xa + n], T[x + "s"][:, xa:xa + n], start, stop),
-             [R(w, wa, wa + 128), R(w + "s", wa, wa + 128), R(x, xa, xa + n)], [R(ps)])
+             [R(w, wa, wa + 128), R(w + "s", wa, wa + 128), R(x, xa, xa + n)], [R(ps)], 0.5 * CYC * (n + 16), pre=pre)
 
-    def dma(q, sem, oap, iap, reads, writes):
-        emit(q, lambda: eng[q].dma_start(oap, iap), reads, writes, sem=sem)
+    def dma(q, sem, oap, iap, reads, writes, lat=1.5):
+        emit(q, lambda: eng[q].dma_start(oap, iap), reads, writes, 0.06, sem=sem, lat=lat)
 
     def sel(o, i, pattern, cmp, fillv, base, cm):
         (oa, orr), (ia, ir) = both(o), both(i)
-        emit("q", lambda: g.affine_select(oa, ia, pattern, cmp, fillv, base, cm), [ir], [orr])
+        emit("q", lambda: g.affine_select(oa, ia, pattern, cmp, fillv, base, cm), [ir], [orr], 0.17 + 2 * CYC * size(o))
 
     def iota(o, pattern, base, cm):
         oa, orr = both(o)
+        cost = 0.13 + 2 * CYC * size(o)
         if SCRATCH[o[0]][2] == "int32":
-            emit("q", lambda: g.iota(oa, pattern, base, cm), [], [orr])
+            emit("q", lambda: g.iota(oa, pattern, base, cm), [], [orr], cost)
         else:
-            emit("q", lambda: g.iota(oa, pattern, base, cm, allow_small_or_imprecise_dtypes=True), [], [orr])
+            emit("q", lambda: g.iota(oa, pattern, base, cm, allow_small_or_imprecise_dtypes=True), [], [orr], cost)
 
     dma("y", "dx0", T.xs[:, 0:1024], T.x[:, 0:1024], [], [R("xs", 0, 1024)])
     dma("s", "du", T.us[:, 0:512], T.u[:, 0:512], [], [R("us")])
-    dma("y", "dx1", T.xs[:, 1024:2048], T.x[:, 1024:2048], [], [R("xs", 1024, 2048)])
-    dma("y", "dwc", T.qw[:, 0:512].bitcast(dt.uint8), T.wc[:, 0:2048], [], [R("qw")])
-    dma("y", "dws", T.qws[:, 0:512], T.ws[:, 0:512], [], [R("qws")])
-    dma("y", "dv", T.vs[:, 0:512], T.v[:, 0:512], [], [R("vs")])
+    dma("y", "dx1", T.xs[:, 1024:2048], T.x[:, 1024:2048], [], [R("xs", 1024, 2048)], lat=2.0)
 
     fill(("one",), 1.0)
     fill(("gw0",), 0.0)
     fill(("nul",), 0.0)
-    fill(("ebt",), 0.0)
+    fill(("prt",), 0.0)
     fill(("ktt",), 0.0)
-    sel(("idm",), ("one",), [[-1, 128]], OP.is_equal, 0.0, 0, 1)
+    fill(("rw", 0, VR), RW)
+    fill(("rw", VR, 140), RS)
+    fill(("neg",), -BIG)
+    for h in (0, 1):
+        dma("y", "dz%d" % h, T.ebt[:, 1024 * h:1024 * h + 1024], T.prt[:, 0:1024], [R("prt")],
+            [R("ebt", 1024 * h, 1024 * h + 1024)], lat=2.5)
+        act(("ebk", 1024 * h, 1024 * h + 1024), ("prt",), ACT.Copy)
+    dma("y", "dwc", T.qw[:, 0:512].bitcast(dt.uint8), T.wc[:, 0:2048], [], [R("qw")], lat=4.0)
+    dma("y", "dws", T.qws[:, 0:512], T.ws[:, 0:512], [], [R("qws")], lat=4.0)
+    dma("y", "dv", T.vs[:, 0:512], T.v[:, 0:512], [], [R("vs")], lat=4.0)
     for i in range(6):
         sel(("gw0",), ("gw0",), [[-16, 8]], OP.not_equal, 2.0 ** (i - 1), -i, 1)
     sel(("gw1",), ("gw0",), [[16, 8]], OP.is_ge, 0.0, 1, -1)
@@ -262,9 +402,10 @@ def rank_program(g, core, T, topo):
     sel(("lod",), ("one",), [[-1, 128]], OP.is_gt, 0.0, 0, 1)
     sel(("lod",), ("lod",), [[-1, 128]], OP.not_equal, -1024.0, 0, 1)
     iota(("kc", 0, 65), [[1, 65]], -32, 0)
+    sel(("blk",), ("one",), [[-16, 8], [0, 16]], OP.is_ge, 0.0, 0, 1)
+    sel(("blk",), ("blk",), [[16, 8], [0, 16]], OP.is_ge, 0.0, 15, -1)
+    sel(("idm",), ("one",), [[-1, 128]], OP.is_equal, 0.0, 0, 1)
     sel(("prm",), ("one",), [[-1, 4], [-4, 32]], OP.is_equal, 0.0, 0, 1)
-    for i in range(6):
-        sel(("krm",), ("krm" if i else "nul",), [[-16, 8], [0, 16]], OP.not_equal, 2.0 ** (i - 1), -i, 1)
     iota(("ip",), [[0, 1]], 0, 1)
     iota(("cneg",), [[-1, 5]], 0, 0)
     iota(("c16",), [[16, 4]], 513, 0)
@@ -276,25 +417,43 @@ def rank_program(g, core, T, topo):
         iota((n, 256, 512), [[0, 256]], 0, 0)
     dma("y", "dlo", T.vals[1:128:16, :], T.lo[1:128:16, :], [R("lo")], [R("vals")])
 
-    def ones_and_zeros(cs):
-        for c in cs:
-            for b in range(4):
-                for s, o in ((0, b < c), (1, b > c)):
-                    if b != c:
-                        act(("lt", 2048 * s + 512 * c + b, 2048 * s + 512 * c + 512, 4), ("one" if o else "nul",), ACT.Copy)
-    ones_and_zeros((0, 1, 2))
     for b in range(4):
         act(("ktt", 5 * b, 128, 16), ("gw0",), ACT.Copy)
         act(("ktt", 128 + 48 + 5 * b, 688, 64), ("gw1",), ACT.Copy, scale=16.0)
         act(("ktt", 688 + 48 + 5 * b, 1248, 64), ("gw2",), ACT.Copy, scale=0.25)
-    fill(("prt",), 0.0)
-    fill(("rw", 0, VR), 1287.5)
-    fill(("rw", VR, 140), 263.5)
+    quant("qk", 0, 312, "ktt", 0, 1248)
     quant("qu", 0, 128, "us", 0, 512)
+    for c in range(4):
+        for s, d in ((0, "upd"), (1, "lod")):
+            for b in range(4):
+                x = ("lt", 2048 * s + 512 * c + b, 2048 * s + 512 * c + 512, 4)
+                w = 0.5 if b == 3 else 1.0
+                if b == c:
+                    vts(x, (d,), w, None, OP.mult)
+                elif c < 3:
+                    fill(x, w if (s == 0) == (b < c) else 0.0)
+                else:
+                    act(x, ("one" if (s == 0) == (b < c) else "nul",), ACT.Copy)
+            quant("ql", 256 + 512 * s + 128 * c, 384 + 512 * s + 128 * c, "lt", 2048 * s + 512 * c, 2048 * s + 512 * c + 512)
+    vreduce(("wcl",), ("gw0",), OP.add)
     for b in range(4):
         vcopy(("ebt", 512 * b + b, 512 * b + 512, 4), ("idm",))
     quant("qe", 0, 512, "ebt", 0, 2048)
-    fill(("neg",), -BIG)
+    for b in range(4):
+        act(("ebk", 512 * b + b, 512 * b + 512, 4), ("blk",), ACT.Identity, scale=("wcl",))
+    quant("qr", 0, 512, "ebk", 0, 2048)
+    act(("prt", 0, 512, 4), ("prm",), ACT.Copy, scale=0.0625)
+    act(("prt", 1, 512, 4), ("prm",), ACT.Copy, scale=32.0)
+    act(("prt", 514, 1024, 4), ("prm",), ACT.Copy)
+    act(("prt", 515, 1024, 4), ("prm",), ACT.Copy)
+    quant("ql", 0, 256, "prt", 0, 1024)
+    vts(("ia",), ("ip",), 15, None, OP.bitwise_and)
+    vcopy(("icf",), ("ia",))
+    vts(("icb",), ("icf",), -4.0, 0.5, OP.mult, OP.add)
+    vts(("tb",), ("cneg",), ("icb",), None, OP.add)
+    vts(("dum",), ("c16",), ("icf",), None, OP.add)
+    fill(("msk0",), BIG)
+    fill(("msk1",), BIG)
 
     lots = ((1, 2, 4, 6), (3, 5, 7))
     near = [x for x in range(1, N) if topo.chip(T.cores[rank ^ x]) == topo.chip(core)]
@@ -307,35 +466,35 @@ def rank_program(g, core, T, topo):
 
     def send(t):
         qa, lc = "qa%d" % t, "lc%d" % t
-        n = need("q", [R(qa)], [])
-        for s in n:
-            wait("q", s, n[s])
+
+        def call(lot, plane):
+            ts = []
+            for group, m in ((far, fmask), (near, nmask)):
+                ids, dsts = [], []
+                for x in lots[lot]:
+                    if x in group:
+                        rid, pid = topo.addr(T.cores[rank ^ x])[:2]
+                        c = 256 * lot + 64 * lots[lot].index(x)
+                        ids.append(DstId(rid=rid, pnc=pid))
+                        dsts.append(T[lc + "s"][:, c:c + 64] if plane else T[lc][:, c:c + 64].bitcast(dt.uint8))
+                if ids:
+                    src = T[qa + "s"][:, 0:64] if plane else T[qa][:, 0:64].bitcast(dt.uint8)
+                    ts.append(RemoteDMATransfer(dst_ids=ids, dma_engine_mask=m, remote_sem=T.sem["%sr%d" % ("ab"[lot], t)],
+                                                srcs=[src], dsts=dsts))
+                    count["sent"] += bin(m).count("1")
+            g.remote_dma_fused(ts, local_sem=T.sem.sent)
         for lot in (0, 1):
             for plane in (0, 1):
-                ts = []
-                for group, m in ((far, fmask), (near, nmask)):
-                    ids, dsts = [], []
-                    for x in lots[lot]:
-                        if x in group:
-                            rid, pid = topo.addr(T.cores[rank ^ x])[:2]
-                            c = 256 * lot + 64 * lots[lot].index(x)
-                            ids.append(DstId(rid=rid, pnc=pid))
-                            dsts.append(T[lc + "s"][:, c:c + 64] if plane else T[lc][:, c:c + 64].bitcast(dt.uint8))
-                    if ids:
-                        src = T[qa + "s"][:, 0:64] if plane else T[qa][:, 0:64].bitcast(dt.uint8)
-                        ts.append(RemoteDMATransfer(dst_ids=ids, dma_engine_mask=m, remote_sem=T.sem["%sr%d" % ("ab"[lot], t)],
-                                                    srcs=[src], dsts=dsts))
-                        count["sent"] += bin(m).count("1")
-                g.remote_dma_fused(ts, local_sem=T.sem.sent)
+                emit("q", lambda lot=lot, plane=plane: call(lot, plane), [R(qa)], [("@q", 1), ("@w%d" % lot, 1)], 0.4, sem="sent")
+            emit("n", None, [("@w%d" % lot, 1)], [R(lc, 256 * lot, 256 + 192 * lot)], 0.0, lat=2.5 + 1.5 * lot)
 
     def ps(i):
         return "ps%d" % i
-    PC0, PC1, HB = [4, 5, 6, 7], [0, 1, 3, 2], {2: 4, 3: 5, 0: 6}
+    HB = {2: 4, 3: 5, 0: 6}
 
     def key_half(t, state, h):
         qx = "qx%d" % t
-        if h or not t:
-            quant(qx, 256 * h, 256 * h + 256, state, 1024 * h, 1024 * h + 1024)
+        quant(qx, 256 * h, 256 * h + 256, state, 1024 * h, 1024 * h + 1024)
         if t < ROUNDS:
             mm(ps(h), 256, "qu", 0, qx, 256 * h)
             act(("bt", 256 * h, 256 * h + 256), (ps(h), 0, 256), ACT.Sign, bias=-(2.0 ** -100))
@@ -349,118 +508,83 @@ def rank_program(g, core, T, topo):
 
     key_half(0, "xs", 0)
     key_half(0, "xs", 1)
-    ones_and_zeros((3,))
-    for c in range(4):
-        vcopy(("lt", 512 * c + c, 512 * c + 512, 4), ("upd",))
-        vcopy(("lt", 2048 + 512 * c + c, 2048 + 512 * c + 512, 4), ("lod",))
     for t in range(ROUNDS):
         qx, qa, lc = "qx%d" % t, "qa%d" % t, "lc%d" % t
         new = "st%d" % (t + 1)
-        if t == 0:
-            quant("qk", 0, 312, "ktt", 0, 1248)
-        mm(ps(4), 512, "qe", 0, qx, 0)
         quant("qb", 0, 128, "bt", 0, 512)
-        mm("ps2", 312, "qb", 0, "qk", 0)
-        for b in (1, 2, 3):
-            mm(ps(4 + b), 512, "qe", 128 * b, qx, 0)
-        if t == 0:
-            fill(("msk0",), BIG)
-        vts(("dd", 0, 512), (ps(4), 0, 512), 0.5, None, OP.mult)
-        for b in (1, 2, 3):
-            act(("dd", 512 * b, 512 * b + 512), (ps(4 + b), 0, 512), ACT.Copy, scale=0.5)
-        if t == 0:
-            quant("ql", 256, 768, "lt", 0, 2048)
-            quant("ql", 768, 1280, "lt", 2048, 4096)
+        mm("ps2", 128, "qb", 0, "qk", 0)
+        mm("ps3", 280, "qb", 0, "qk", 32)
+        act(("tt", 2, 560, 4), ("ps3", 0, 140), ACT.Copy)
+        act(("tt", 3, 560, 4), ("ps3", 140, 280), ACT.Copy)
+        for b in range(4):
+            mm(ps(6 + b % 2), 512, "qe", 128 * b, qx, 0)
+            act(("dd", 512 * b, 512 * b + 512), (ps(6 + b % 2), 0, 512), ACT.Copy, scale=0.5)
+        act(("kng",), ("ps2", 3, 32, 4), ACT.Copy, scale=-1.0)
         for h in (0, 1):
-            for b in range(4):
-                for gg in range(4):
-                    c = 4 * (4 * h + gg) + b
-                    vts(("ot", 1040 * h + 4 * gg + b, 1040 * h + 1040, 16), ("kc", 0, 65), ("ps2", c, c + 1), None, OP.is_gt)
-            quant("qo", 260 * h, 260 * h + 260, "ot", 1040 * h, 1040 * h + 1040)
-            if h == 0:
-                for c in range(4):
-                    mm(ps(PC0[c]), 256, "ql", 256 + 128 * c, "qo", 4, True, False)
-                    mm(ps(PC0[c]), 256, "ql", 768 + 128 * c, "qo", 0, False, True)
-        if t == 0:
-            act(("prt", 0, 512, 4), ("prm",), ACT.Copy, scale=0.0625)
-            act(("prt", 1, 512, 4), ("prm",), ACT.Copy, scale=32.0)
-            act(("prt", 514, 1024, 4), ("prm",), ACT.Copy)
-            act(("prt", 515, 1024, 4), ("prm",), ACT.Copy)
-        act(("tt", 2, 560, 4), ("ps2", 32, 172), ACT.Copy)
-        act(("tt", 3, 560, 4), ("ps2", 172, 312), ACT.Copy)
-        for c in range(4):
-            mm(ps(PC1[c]), 256, "ql", 256 + 128 * c, "qo", 264, True, False)
-            mm(ps(PC1[c]), 256, "ql", 768 + 128 * c, "qo", 260, False, True)
-        for c in range(4):
             for gg in range(4):
-                k = 12 + 16 * gg + c
-                vmax(("rw", k, k + 1), (ps(PC0[c]), gg, 256, 4))
-        for c in range(4):
-            for gg in range(GV - 4, 4):
-                k, z = 76 + 16 * gg + c, 64 * (gg + 4 * (c % 2))
-                act(("sj", z, z + 64), (ps(PC1[c]), gg, 256, 4), ACT.Relu, bias=-1024.0, accum=("rw", k, k + 1))
-            for gg in range(GV - 4):
-                k = 76 + 16 * gg + c
-                vmax(("rw", k, k + 1), (ps(PC1[c]), gg, 256, 4))
-        act(("rv", VR, 140), ("rw", VR, 140), ACT.Identity, bias=-263.5)
-        vts(("rv", 0, VR), ("rw", 0, VR), 1287.5, None, OP.subtract)
-        if t == 0:
-            quant("ql", 0, 256, "prt", 0, 1024)
-        vts(("tt", 0, 560, 4), ("rv",), MAGIC, MAGIC, OP.add, OP.subtract)
-        vtt(("tt", 1, 560, 4), ("rv",), ("tt", 0, 560, 4), OP.subtract)
+                for b in range(4):
+                    c = 4 * (4 * h + gg) + b
+                    o = ("ot", 1040 * h + 4 * gg + b, 1040 * h + 1040, 16)
+                    if b == 3:
+                        act(o, ("kc", 0, 65), ACT.Sign, bias=("kng", c // 4, c // 4 + 1))
+                    else:
+                        vts(o, ("kc", 0, 65), ("ps2", c, c + 1), 0.5, OP.is_gt, OP.subtract)
+            quant("qo", 260 * h, 260 * h + 260, "ot", 1040 * h, 1040 * h + 1040)
+        for b in range(4):
+            mm("ps3", 128, "qr", 128 * b, "qb", 0)
+            act(("kf", b, 512, 4), ("ps3", 0, 128), ACT.Identity, bias=31.5)
+        for c in range(5):
+            act(("jk", 512 * c, 512 * c + 512), ("kf",), ACT.Sign, bias=("tb", c, c + 1), accum=("acc", c, c + 1))
+        act(("b5",), ("acc",), ACT.Copy, bias=256.0, scale=-0.5, lat=0.8)
+        dma("y", "dk%d" % t, T.kl[8 * t:8 * t + 8, :], T.kf[0:128:16, :], [R("kf")], [])
+        for h in (0, 1):
+            for c in range(4):
+                p = ps(((0, 1, 4, 5), (0, 1, 4, 2))[h][c])
+                mm(p, 256, "ql", 256 + 128 * c, "qo", 260 * h + 4, True, False)
+                mm(p, 256, "ql", 768 + 128 * c, "qo", 260 * h, False, True)
+                for gg in range(4):
+                    k = 12 + 16 * (4 * h + gg) + c
+                    if k < VR:
+                        vreduce(("rw", k, k + 1), (p, gg, 256, 4), OP.max)
+                    else:
+                        z = 64 * (2 * c + gg - 2)
+                        act(("sj", z, z + 64), (p, gg, 256, 4), ACT.Relu, bias=-512.0, accum=("rw", k, k + 1))
+        for o in ("hi", "rv"):
+            vts((o, 0, VR), ("rw", 0, VR), M16 - RW, None, OP.add)
+            act((o, VR, 140), ("rw", VR, 140), ACT.Identity, bias=M16 - RS)
+        vts(("tt", 0, 560, 4), ("hi",), M16, None, OP.subtract)
+        vtt(("tt", 1, 560, 4), ("rv",), ("hi",), OP.subtract)
         quant("qt", 0, 140, "tt", 0, 560)
-
-        def group_keys():
-            for b in range(4):
-                mm(ps((0, 1, 3, 2)[b]), 128, "qr", 128 * b, "qb", 0)
-            for b in range(4):
-                act(("kf", b, 512, 4), (ps((0, 1, 3, 2)[b]), 0, 128), ACT.Identity, bias=31.5)
-            for c in range(5):
-                act(("ge", 512 * c, 512 * c + 512) if c < 4 else ("sj",), ("kf",), ACT.Sign, bias=("tb", c, c + 1),
-                    accum=("acc", c, c + 1))
-            act(("b5",), ("acc",), ACT.Copy, bias=256.0, scale=-0.5)
-            dma("y", "dk%d" % t, T.kl[8 * t:8 * t + 8, :], T.kf[0:128:16, :], [R("kf")], [])
-
-        if t:
-            group_keys()
         for q in range(4):
-            mm("ps4", 128, "qt", 12 - 4 * q, "ql", 32 * q, q == 0, q == 3)
+            mm("ps0", 128, "qt", 12 - 4 * q, "ql", 32 * q, q == 0, q == 3)
         for q in range(4):
-            mm("ps5", 128, "qt", 12 - 4 * q, "ql", 128 + 32 * q, q == 0, q == 3)
-        if t == 0:
-            for b in range(4):
-                act(("ebt", 512 * b + b, 512 * b + 512, 4), ("krm",), ACT.Copy)
-            quant("qr", 0, 512, "ebt", 0, 2048)
-        vts(("po",), ("ps4", 0, 32), 256.0, None, OP.add)
-        if t == 0:
-            vts(("ia",), ("ip",), 15, None, OP.bitwise_and)
-            vcopy(("icf",), ("ia",))
-            vts(("icb",), ("icf",), -4.0, 0.5, OP.mult, OP.add)
-            vts(("tb",), ("cneg",), ("icb",), None, OP.add)
-            vts(("dum",), ("c16",), ("icf",), None, OP.add)
-            group_keys()
-        vscatter(("lsw",), ("vals",), ("po",))
-        vtrans(("ltr",), ("lsw",))
-        for gg in (0, 1):
-            vtt(("lj", 16 * gg, 16 * gg + 16), ("ltr", 16 * gg, 512, 32), ("ltr", 16 * gg + 1, 512, 32), OP.add)
-        vtrans(("lk",), ("lj",))
-        vcopy(("l16",), ("lk",))
-        for b in (1, 2, 3):
-            act(("sd", 512 * b, 512 * b + 512), ("dd", 512 * b, 512 * b + 512), ACT.Copy, off=("l16",))
-        vgather(("sd", 0, 512), ("dd", 0, 512), ("l16",))
+            mm("ps1", 128, "qt", 12 - 4 * q, "ql", 128 + 32 * q, q == 0, q == 3)
+        vts(("po",), ("ps0", 0, 32), 256.0, None, OP.add)
+        vts(("ko",), ("ps1", 0, 32), 31.5, None, OP.add)
         msk = "msk%d" % t
         vtt(("em",), ("b5", 1, 5), ("b5", 0, 4), OP.is_equal)
-        vts(("ko",), ("ps5", 0, 32), 31.5, None, OP.add)
         vtt(("dm",), ("em",), ("dum",), OP.mult)
         vtt(("mk",), ("b5", 0, 4), ("dm",), OP.max)
         vtt(("pk",), ("b5", 1, 5), ("dm",), OP.max)
         vcopy(("mk16",), ("mk",))
         vts(("pk16",), ("pk",), 1.0, None, OP.subtract)
         vscatter((msk,), ("neg",), ("mk16",))
-        for b in range(4):
+        vscatter(("lsw",), ("vals",), ("po",))
+        vtrans(("ltr",), ("lsw",))
+        for gg in (0, 1):
+            vtt(("lj", 16 * gg, 16 * gg + 16), ("ltr", 16 * gg, 512, 32), ("ltr", 16 * gg + 1, 512, 32), OP.add)
+        vtrans(("lk",), ("lj",))
+        vcopy(("l16",), ("lk",))
+        for b in (0, 2, 1, 3):
+            o, i = ("sd", 512 * b, 512 * b + 512), ("dd", 512 * b, 512 * b + 512)
+            if b < 2:
+                vgather(o, i, ("l16",))
+            else:
+                act(o, i, ACT.Copy, off=("l16",))
+        for b in (0, 2, 1, 3):
             vscan(("sc", 576 * b, 576 * b + 512), (msk, 0, 512), ("sd", 512 * b, 512 * b + 512))
             o, i = ("at", b, 256, 4), ("sc", 576 * b, 576 * b + 576)
-            if b in (1, 2):
+            if b < 3:
                 act(o, i, ACT.Copy, scale=2.0, off=("pk16",))
             else:
                 vts(o, i, 2.0, None, OP.mult, off=("pk16",))
@@ -475,19 +599,16 @@ def rank_program(g, core, T, topo):
                 act(("ebt", 512 * b + b, 512 * b + 512, 4), ("idm",), ACT.Copy, scale=0.5)
             quant("qv", 0, 128, "vs", 0, 512)
             quant("qh", 0, 512, "ebt", 0, 2048)
-            fill(("msk1",), BIG)
-        wait("t", "ar%d" % t, arrive(0))
+        for b in (2, 3, 0):
+            mm(ps(HB[b]), 512, "qh", 128 * b, qx, 0)
         for b in range(4):
-            mm(ps(4 + b), 256, "qe", 128 * b, lc, 0)
+            mm(ps(b), 256, "qe", 128 * b, lc, 0, pre=[("ar%d" % t, arrive(0))])
         for s in range(4):
             for b in range(4):
                 o, w = ("mm", 64 * b, 64 * b + 64), ("own" if s == 0 else "mm", 64 * b, 64 * b + 64)
-                vtt(o, (ps(4 + b), 64 * s, 64 * s + 64), w, OP.max)
-        for b in (2, 3, 0):
-            mm(ps(HB[b]), 512, "qh", 128 * b, qx, 0)
-        wait("t", "br%d" % t, arrive(1))
+                vtt(o, (ps(b), 64 * s, 64 * s + 64), w, OP.max)
         for b in range(4):
-            mm(ps(b), 192, "qe", 128 * b, lc, 256)
+            mm(ps(b), 192, "qe", 128 * b, lc, 256, pre=[("br%d" % t, arrive(1))])
         for s in range(3):
             for b in range(4):
                 w = ("mm", 64 * b, 64 * b + 64)
@@ -496,11 +617,7 @@ def rank_program(g, core, T, topo):
         for b in range(4):
             mm(ps(b), 128, "qw", 128 * b, "qz", 0)
         for b in range(4):
-            o, i = ("gt", b, 256, 4), (ps(b), 0, 64)
-            if b % 2:
-                act(o, i, ACT.Relu, scale=0.015625)
-            else:
-                vts(o, i, 0.0, 0.015625, OP.max, OP.mult)
+            vts(("gt", b, 256, 4), (ps(b), 0, 64), 0.0, 0.015625, OP.max, OP.mult)
         quant("qg", 0, 128, "gt", 0, 512)
         for b in (0, 2, 1, 3):
             mm(ps(b), 128, "qe", 128 * b, "qg", 0)
@@ -521,14 +638,16 @@ def rank_program(g, core, T, topo):
                     vtt(o, (ps(HB[b]), 256 * h, 256 * h + 256), ("ge", 1024 * h + 256 * b, 1024 * h + 256 * b + 256), OP.add)
                 else:
                     vtt(o, ("gb", 64 * b, 64 * b + 64), ("dd", 512 * b + 256 * h, 512 * b + 256 * h + 256), OP.add, off=off)
-            if h == 0:
-                quant("qx%d" % (t + 1), 0, 256, new, 0, 1024)
         for h in (0, 1):
             key_half(t + 1, new, h)
 
     qx = "qx%d" % ROUNDS
     for k in range(4):
         dma("y", "ds", T.osc[4 * k:4 * k + 4, :], T[qx + "s"][32 * k:32 * k + 4, :], [R(qx)], [])
+    if not _PLAN:
+        _PLAN.extend(plan(ops, TRIES))
+    for i in _PLAN:
+        issue(ops[i])
     count["ar0"] = count["ar1"] = arrive(0)
     count["br0"] = count["br1"] = arrive(1)
     for s in SEMAPHORES:

from concourse.bass import DstId, RemoteDMATransfer
from concourse.mybir import dt, AluOpType, AxisListType, ActivationFunctionType

OP, ACT, AX = AluOpType, ActivationFunctionType, AxisListType
ROUNDS = 2
BIG = 2.0 ** 60
M16 = 3072.0
TRIES = 24
VR = 108
RW = 1032.0
RS = 520.0

SCRATCH = {}


def _b(names, n, dtype="bfloat16"):
    for name in names.split():
        SCRATCH[name] = ("sbuf", [128, n], dtype)


def _codes(names, n):
    for name in names.split():
        SCRATCH[name] = ("sbuf", [128, n], "float8_e4m3fn_x4")
        SCRATCH[name + "s"] = ("sbuf", [128, n], "uint8")


_b("xs st1 st2 ebt ebk dd sd ge", 2048)
_b("us vs bt at zt gt vals lo lsw ltr sj", 512)
_b("jk", 2560)
_b("one nul idm blk upd lod prm", 128)
_b("gw0 gw1 gw2", 8)
_b("kc", 66)
_b("ktt", 1248)
_b("lt", 4096)
_b("prt", 1024)
_b("ot", 2080)
_b("tt", 560)
_b("msk0 msk1", 592)
_b("sc", 2304)
_b("neg", 64)
_b("own mm gb", 256)
_b("hi", 140)
_b("rw rv", 140, "float32")
_b("kf yb", 512, "float32")
_b("lj lk", 32, "float32")
_b("kng", 8, "float32")
_b("acc b5 cneg tb", 5, "float32")
_b("em dm mk pk dum c16", 4, "float32")
_b("icf icb wcl", 1, "float32")
_b("ip ia", 1, "int32")
_b("po ko l16", 32, "uint16")
_b("mk16 pk16", 4, "uint16")
_codes("qu qv qb qa0 qa1 qz qg", 128)
_codes("qx0 qx1 qx2 qw qe qh qr", 512)
_codes("qk", 312)
_codes("ql", 1280)
_codes("qo", 520)
_codes("qt", 140)
_codes("lc0 lc1", 448)
for _i in range(8):
    SCRATCH["ps%d" % _i] = ("psum", [128, 512], "float32")

SEMAPHORES = ["cv", "cs", "ct", "cq", "ar0", "ar1", "br0", "br1", "sent",
              "dx0", "dx1", "du", "dv", "dwc", "dws", "dlo", "dz0", "dz1", "dk0", "dk1", "dy0", "dy1", "do0", "do1", "ds"]

_MASKS = {}
_PLAN = []


def _cols(a, b, st):
    if (a, b, st) not in _MASKS:
        m = 0
        for i in range(a, b, st):
            m |= 1 << i
        _MASKS[(a, b, st)] = m
    return _MASKS[(a, b, st)]


def plan(ops, tries):
    wr, rd, pred = {}, {}, []
    for i, o in enumerate(ops):
        p = set()
        for name, m in o["reads"]:
            for wm, j in wr.get(name, []):
                if wm & m:
                    p.add(j)
            if name[:2] == "ps":
                for rm, j in rd.get(name, []):
                    if ops[j]["e"] != o["e"]:
                        p.add(j)
        for name, m in o["writes"]:
            for om, j in wr.get(name, []) + rd.get(name, []):
                if om & m:
                    p.add(j)
        p.discard(i)
        for name, m in o["writes"]:
            wr[name] = [w for w in wr.get(name, []) if w[0] & ~m] + [(m, i)]
            rd[name] = [r for r in rd.get(name, []) if r[0] & ~m]
        for name, m in o["reads"]:
            rd[name] = rd.get(name, []) + [(m, i)]
        pred.append(sorted(p))
    n = len(ops)
    every = range(n)
    succ = [[] for _ in ops]
    for i in every:
        for j in pred[i]:
            succ[j].append(i)
    eng = [o["e"] for o in ops]
    hold = [o["hold"] for o in ops]
    lat = [o["lat"] for o in ops]
    WAKE = 0.18

    def free_of(j, i):
        return eng[j] == "t" and eng[i] == "t" or eng[i] == "n"

    def gap(j, i):
        return lat[j] if free_of(j, i) else lat[j] + WAKE

    def place(order, early):
        t = [0.0] * n
        busy = {e: [] for e in eng}
        for i in order:
            d = hold[i]
            if early:
                lo = max([0.0] + [t[j] + gap(j, i) for j in pred[i]])
            else:
                lo = max([lat[i]] + [t[k] + gap(i, k) for k in succ[i]]) - d
            if eng[i] != "n":
                b = busy[eng[i]]
                z = len(b)
                while z and b[z - 1][1] > lo + 1e-9:
                    z -= 1
                while z < len(b) and b[z][0] < lo + d - 1e-9:
                    lo = max(lo, b[z][1])
                    z += 1
                b.insert(z, (lo, lo + d))
            t[i] = lo if early else lo + d
        return t

    def run(order, tensor, wake, others):
        t = [0.0] * n
        free = {}
        end = 0.0
        for i in order:
            s = free.get(eng[i], 0.0)
            for j in pred[i]:
                x = t[j] if free_of(j, i) else t[j] + wake
                if x > s:
                    s = x
            f = tensor if eng[i] == "t" else others if eng[i] == "n" else 1.0
            if eng[i] != "n":
                free[eng[i]] = s + hold[i] * f
            t[i] = s + lat[i] * f
            end = max(end, t[i])
        return end
    best, seed = None, 1
    for k in range(tries):
        way = [0.0] * n
        for i in range(n - 1, -1, -1):
            seed = (seed * 1103515245 + 12345) % 2147483648
            w = lat[i] * (1.0 + (0.8 * seed / 2147483648 - 0.4 if k else 0.0))
            way[i] = max([w] + [w + gap(i, x) - lat[i] + way[x] for x in succ[i]])
        t = place(sorted(every, key=lambda i: (-way[i], i)), True)
        for _ in range(3):
            order = sorted(every, key=lambda i: (t[i], i))
            score = sum(run(order, *v) for v in ((1.0, 0.1, 1.0), (1.0, 0.18, 1.3), (2.0, 0.18, 1.0), (1.0, 0.25, 0.8)))
            if best is None or score < best[0]:
                best = (score, order)
            late = place(sorted(every, key=lambda i: (-(t[i] + lat[i]), -i)), False)
            t = place(sorted(every, key=lambda i: (-late[i], i)), True)
    return best[1]


def prog(g, T):
    eng = {"v": g.vector, "s": g.scalar, "t": g.tensor, "q": g, "y": g.sync}
    csem = {"v": "cv", "s": "cs", "t": "ct", "q": "cq"}
    count = {s: 0 for s in SEMAPHORES}
    known = {e: {} for e in eng}
    snap = {}
    wr, rd = {}, {}

    def wait(e, sem, val):
        if known[e].get(sem, 0) < val:
            eng[e].wait_ge(T.sem[sem], val)
            for s, k in snap.get((sem, val), {}).items():
                if known[e].get(s, 0) < k:
                    known[e][s] = k
            known[e][sem] = val

    def need(e, reads, writes):
        n = {}

        def add(tok):
            if n.get(tok[0], 0) < tok[1]:
                n[tok[0]] = tok[1]
        for name, m in reads:
            psum = name[:2] == "ps"
            for wm, tok, we in wr.get(name, []):
                if wm & m and not (psum and we == e):
                    add(tok)
            if psum:
                for rm, tok, re_ in rd.get(name, []):
                    if re_ != e:
                        add(tok)
        for name, m in writes:
            for om, tok, oe in wr.get(name, []) + rd.get(name, []):
                if om & m and not (e == "t" and oe == "t"):
                    add(tok)
        return n

    def note(e, reads, writes, tok):
        for name, m in writes:
            wr[name] = [w for w in wr.get(name, []) if w[0] & ~m] + [(m, tok, e)]
            rd[name] = [r for r in rd.get(name, []) if r[0] & ~m]
        for name, m in reads:
            rd[name] = [r for r in rd.get(name, [])
                        if not (r[2] == e and e != "dma" and r[0] & ~m == 0)] + [(m, tok, e)]

    def issue(o):
        e = o["e"]
        if e == "n":
            return
        reads = [r for r in o["reads"] if r[0][0] != "@"]
        writes = [w for w in o["writes"] if w[0][0] != "@"]
        for s, v in o["pre"]:
            wait(e, s, v)
        n = need(e, reads, writes)
        for s in sorted(n, key=lambda s: -n[s]):
            wait(e, s, n[s])
        if o["sem"] == "sent":
            o["call"]()
            return
        s = o["sem"] or csem[e]
        k = 16 if o["sem"] else 1
        o["call"]().then_inc(T.sem[s], k)
        count[s] += k
        snap[(s, count[s])] = dict(known[e])
        note("dma" if o["sem"] else e, reads, writes, (s, count[s]))
    return eng, count, wait, issue


def rank_program(g, core, T, topo):
    rank = T.rank_of(core)
    if rank is None:
        return
    N = len(T.cores)
    eng, count, wait, issue = prog(g, T)
    V, S, PE = g.vector, g.scalar, g.tensor
    ops = []
    CYC = 0.00083

    def emit(e, call, reads, writes, cost, sem=None, lat=None, pre=()):
        ops.append({"e": e, "call": call, "reads": reads, "writes": writes, "sem": sem, "pre": list(pre),
                    "hold": cost, "lat": cost if lat is None else lat})

    def R(name, a=0, b=None, st=1):
        if name[:2] == "ps":
            return (name, 1)
        return (name, _cols(a, SCRATCH[name][1][1] if b is None else b, st))

    def A(name, a=0, b=None, st=1):
        b = SCRATCH[name][1][1] if b is None else b
        return T[name][:, a:b] if st == 1 else T[name][:, a:b:st]

    def both(x):
        return A(*x), R(*x)

    def size(x):
        return len(range(x[1] if len(x) > 1 else 0, x[2] if len(x) > 2 else SCRATCH[x[0]][1][1], x[3] if len(x) > 3 else 1))

    def vcost(*xs, half=True):
        short = all(SCRATCH[x[0]][2] in ("bfloat16", "uint16") for x in xs)
        return 0.05 + CYC * max(64, max(size(x) for x in xs) * (0.5 if short and half else 1.0))

    def fill(x, c):
        a, r = both(x)
        emit("v", lambda: V.memset(a, c), [], [r], vcost(x))

    def vcopy(o, i):
        (oa, orr), (ia, ir) = both(o), both(i)
        emit("v", lambda: V.tensor_copy(oa, ia), [ir], [orr], vcost(o, i))

    def vts(o, i, s1, s2, op0, op1=None, off=None):
        (oa, orr), (ia, ir) = both(o), both(i)
        rs = [ir]
        if isinstance(s1, tuple):
            s1, r1 = both(s1)
            rs.append(r1)
        cost = vcost(o, i)
        if off:
            fa, fr = both(off)
            ia = ia.indirect(fa)
            rs.append(fr)
            cost = 0.05 + 1.5 * CYC * size(o)
        if op1 is None:
            emit("v", lambda: V.tensor_scalar(oa, ia, s1, None, op0), rs, [orr], cost)
        else:
            emit("v", lambda: V.tensor_scalar(oa, ia, s1, s2, op0, op1), rs, [orr], cost)

    def vtt(o, i0, i1, op, off=None):
        (oa, orr), (a0, r0), (a1, r1) = both(o), both(i0), both(i1)
        rs = [r0, r1]
        cost = vcost(o, i1, half=False)
        if off:
            fa, fr = both(off)
            a0 = a0.indirect(fa)
            rs.append(fr)
            cost = 0.05 + 1.5 * CYC * size(o)
        emit("v", lambda: V.tensor_tensor(oa, a0, a1, op), rs, [orr], cost)

    def vscan(o, mask, data):
        (oa, orr), (ma, mr), (da, dr) = both(o), both(mask), both(data)
        emit("v", lambda: V.tensor_tensor_scan(oa, ma, da, -BIG, OP.min, OP.max), [mr, dr], [orr], vcost(o, data))

    def vgather(o, i, off):
        (oa, orr), (ia, ir), (fa, fr) = both(o), both(i), both(off)
        emit("v", lambda: V.tensor_copy(oa, ia.indirect(fa)), [ir, fr], [orr], 0.05 + 1.5 * CYC * size(o))

    def vscatter(o, i, off):
        (oa, orr), (ia, ir), (fa, fr) = both(o), both(i), both(off)
        emit("v", lambda: V.tensor_copy(oa.indirect(fa), ia), [ir, fr], [orr], 0.05 + 3.0 * CYC * size(i))

    def vtrans(o, i):
        (oa, orr), (ia, ir) = both(o), both(i)
        emit("v", lambda: V.transpose(oa, ia), [ir], [orr], vcost(o, i))

    def vreduce(o, i, op):
        (oa, orr), (ia, ir) = both(o), both(i)
        emit("v", lambda: V.tensor_reduce(oa, ia, AX.X, op), [ir], [orr], vcost(i, half=False))

    def quant(q, a, b, x, xa, xb):
        emit("v", lambda: V.quantize_mx(T[q][:, a:b], T[q + "s"][:, a:b], T[x][:, xa:xb]),
             [R(x, xa, xb)], [R(q, a, b)], 0.012 + 0.00022 * (xb - xa))

    def act(o, i, f, bias=0.0, scale=1.0, off=None, accum=None, lat=None):
        (oa, orr), (ia, ir) = both(o), both(i)
        rs, ws = [ir], [orr]
        if isinstance(bias, tuple):
            bias, r1 = both(bias)
            rs.append(r1)
        if isinstance(scale, tuple):
            scale, r1 = both(scale)
            rs.append(r1)
        cost = 0.065 + CYC * size(o)
        if off:
            fa, fr = both(off)
            ia = ia.indirect(fa)
            rs.append(fr)
            cost = 0.065 + 1.5 * CYC * size(o)
        if accum:
            aa, ar = both(accum)
            ws.append(ar)
            emit("s", lambda: S.activation(oa, ia, f, bias=bias, scale=scale, accum_out=aa), rs, ws, cost + 0.02)
        else:
            emit("s", lambda: S.activation(oa, ia, f, bias=bias, scale=scale), rs, ws, cost, lat=lat)

    def mm(ps, n, w, wa, x, xa, start=True, stop=True, pre=()):
        emit("t", lambda: PE.matmul_mx(T[ps][:, 0:n], T[w][:, wa:wa + 128], T[w + "s"][:, wa:wa + 128],
                                       T[x][:, xa:xa + n], T[x + "s"][:, xa:xa + n], start, stop),
             [R(w, wa, wa + 128), R(w + "s", wa, wa + 128), R(x, xa, xa + n)], [R(ps)], 0.5 * CYC * (n + 16), pre=pre)

    def dma(q, sem, oap, iap, reads, writes, lat=1.5):
        emit(q, lambda: eng[q].dma_start(oap, iap), reads, writes, 0.06, sem=sem, lat=lat)

    def sel(o, i, pattern, cmp, fillv, base, cm):
        (oa, orr), (ia, ir) = both(o), both(i)
        emit("q", lambda: g.affine_select(oa, ia, pattern, cmp, fillv, base, cm), [ir], [orr], 0.17 + 2 * CYC * size(o))

    def iota(o, pattern, base, cm):
        oa, orr = both(o)
        cost = 0.13 + 2 * CYC * size(o)
        if SCRATCH[o[0]][2] == "int32":
            emit("q", lambda: g.iota(oa, pattern, base, cm), [], [orr], cost)
        else:
            emit("q", lambda: g.iota(oa, pattern, base, cm, allow_small_or_imprecise_dtypes=True), [], [orr], cost)

    dma("y", "dx0", T.xs[:, 0:1024], T.x[:, 0:1024], [], [R("xs", 0, 1024)])
    dma("s", "du", T.us[:, 0:512], T.u[:, 0:512], [], [R("us")])
    dma("y", "dx1", T.xs[:, 1024:2048], T.x[:, 1024:2048], [], [R("xs", 1024, 2048)], lat=2.0)

    fill(("one",), 1.0)
    fill(("gw0",), 0.0)
    fill(("nul",), 0.0)
    fill(("prt",), 0.0)
    fill(("ktt",), 0.0)
    fill(("rw", 0, VR), RW)
    fill(("rw", VR, 140), RS)
    fill(("neg",), -BIG)
    for h in (0, 1):
        dma("y", "dz%d" % h, T.ebt[:, 1024 * h:1024 * h + 1024], T.prt[:, 0:1024], [R("prt")],
            [R("ebt", 1024 * h, 1024 * h + 1024)], lat=2.5)
        act(("ebk", 1024 * h, 1024 * h + 1024), ("prt",), ACT.Copy)
    dma("y", "dwc", T.qw[:, 0:512].bitcast(dt.uint8), T.wc[:, 0:2048], [], [R("qw")], lat=4.0)
    dma("y", "dws", T.qws[:, 0:512], T.ws[:, 0:512], [], [R("qws")], lat=4.0)
    dma("y", "dv", T.vs[:, 0:512], T.v[:, 0:512], [], [R("vs")], lat=4.0)
    for i in range(6):
        sel(("gw0",), ("gw0",), [[-16, 8]], OP.not_equal, 2.0 ** (i - 1), -i, 1)
    sel(("gw1",), ("gw0",), [[16, 8]], OP.is_ge, 0.0, 1, -1)
    sel(("gw2",), ("gw0",), [[-16, 8]], OP.is_ge, 0.0, -2, 1)
    sel(("upd",), ("one",), [[1, 128]], OP.is_gt, 0.0, 0, -1)
    sel(("upd",), ("upd",), [[1, 128]], OP.not_equal, 1024.0, 0, -1)
    sel(("lod",), ("one",), [[-1, 128]], OP.is_gt, 0.0, 0, 1)
    sel(("lod",), ("lod",), [[-1, 128]], OP.not_equal, -1024.0, 0, 1)
    iota(("kc", 0, 65), [[1, 65]], -32, 0)
    sel(("blk",), ("one",), [[-16, 8], [0, 16]], OP.is_ge, 0.0, 0, 1)
    sel(("blk",), ("blk",), [[16, 8], [0, 16]], OP.is_ge, 0.0, 15, -1)
    sel(("idm",), ("one",), [[-1, 128]], OP.is_equal, 0.0, 0, 1)
    sel(("prm",), ("one",), [[-1, 4], [-4, 32]], OP.is_equal, 0.0, 0, 1)
    iota(("ip",), [[0, 1]], 0, 1)
    iota(("cneg",), [[-1, 5]], 0, 0)
    iota(("c16",), [[16, 4]], 513, 0)
    iota(("lo",), [[0, 2], [1, 256]], 0, 0)
    iota(("vals",), [[256, 2], [0, 256]], 0, 0)
    for b in range(4):
        iota(("sc", 576 * b + 512, 576 * b + 576), [[0, 64]], 0, 0)
    for n in ("at", "zt", "gt"):
        iota((n, 256, 512), [[0, 256]], 0, 0)
    dma("y", "dlo", T.vals[1:128:16, :], T.lo[1:128:16, :], [R("lo")], [R("vals")])

    for b in range(4):
        act(("ktt", 5 * b, 128, 16), ("gw0",), ACT.Copy)
        act(("ktt", 128 + 48 + 5 * b, 688, 64), ("gw1",), ACT.Copy, scale=16.0)
        act(("ktt", 688 + 48 + 5 * b, 1248, 64), ("gw2",), ACT.Copy, scale=0.25)
    quant("qk", 0, 312, "ktt", 0, 1248)
    quant("qu", 0, 128, "us", 0, 512)
    for c in range(4):
        for s, d in ((0, "upd"), (1, "lod")):
            for b in range(4):
                x = ("lt", 2048 * s + 512 * c + b, 2048 * s + 512 * c + 512, 4)
                w = 0.5 if b == 3 else 1.0
                if b == c:
                    vts(x, (d,), w, None, OP.mult)
                elif c < 3:
                    fill(x, w if (s == 0) == (b < c) else 0.0)
                else:
                    act(x, ("one" if (s == 0) == (b < c) else "nul",), ACT.Copy)
            quant("ql", 256 + 512 * s + 128 * c, 384 + 512 * s + 128 * c, "lt", 2048 * s + 512 * c, 2048 * s + 512 * c + 512)
    vreduce(("wcl",), ("gw0",), OP.add)
    for b in range(4):
        vcopy(("ebt", 512 * b + b, 512 * b + 512, 4), ("idm",))
    quant("qe", 0, 512, "ebt", 0, 2048)
    for b in range(4):
        act(("ebk", 512 * b + b, 512 * b + 512, 4), ("blk",), ACT.Identity, scale=("wcl",))
    quant("qr", 0, 512, "ebk", 0, 2048)
    act(("prt", 0, 512, 4), ("prm",), ACT.Copy, scale=0.0625)
    act(("prt", 1, 512, 4), ("prm",), ACT.Copy, scale=32.0)
    act(("prt", 514, 1024, 4), ("prm",), ACT.Copy)
    act(("prt", 515, 1024, 4), ("prm",), ACT.Copy)
    quant("ql", 0, 256, "prt", 0, 1024)
    vts(("ia",), ("ip",), 15, None, OP.bitwise_and)
    vcopy(("icf",), ("ia",))
    vts(("icb",), ("icf",), -4.0, 0.5, OP.mult, OP.add)
    vts(("tb",), ("cneg",), ("icb",), None, OP.add)
    vts(("dum",), ("c16",), ("icf",), None, OP.add)
    fill(("msk0",), BIG)
    fill(("msk1",), BIG)

    lots = ((1, 2, 4, 6), (3, 5, 7))
    near = [x for x in range(1, N) if topo.chip(T.cores[rank ^ x]) == topo.chip(core)]
    far = [x for x in range(1, N) if x not in near]
    fmask = topo.mask(core, T.cores[rank ^ far[0]])
    nmask = topo.mask(core, T.cores[rank ^ near[0]]) & ~fmask

    def arrive(lot):
        return sum(2 * bin(nmask if x in near else fmask).count("1") for x in lots[lot])

    def send(t):
        qa, lc = "qa%d" % t, "lc%d" % t

        def call(lot, plane):
            ts = []
            for group, m in ((far, fmask), (near, nmask)):
                ids, dsts = [], []
                for x in lots[lot]:
                    if x in group:
                        rid, pid = topo.addr(T.cores[rank ^ x])[:2]
                        c = 256 * lot + 64 * lots[lot].index(x)
                        ids.append(DstId(rid=rid, pnc=pid))
                        dsts.append(T[lc + "s"][:, c:c + 64] if plane else T[lc][:, c:c + 64].bitcast(dt.uint8))
                if ids:
                    src = T[qa + "s"][:, 0:64] if plane else T[qa][:, 0:64].bitcast(dt.uint8)
                    ts.append(RemoteDMATransfer(dst_ids=ids, dma_engine_mask=m, remote_sem=T.sem["%sr%d" % ("ab"[lot], t)],
                                                srcs=[src], dsts=dsts))
                    count["sent"] += bin(m).count("1")
            g.remote_dma_fused(ts, local_sem=T.sem.sent)
        for lot in (0, 1):
            for plane in (0, 1):
                emit("q", lambda lot=lot, plane=plane: call(lot, plane), [R(qa)], [("@q", 1), ("@w%d" % lot, 1)], 0.4, sem="sent")
            emit("n", None, [("@w%d" % lot, 1)], [R(lc, 256 * lot, 256 + 192 * lot)], 0.0, lat=2.5 + 1.5 * lot)

    def ps(i):
        return "ps%d" % i
    HB = {2: 4, 3: 5, 0: 6}

    def key_half(t, state, h):
        qx = "qx%d" % t
        quant(qx, 256 * h, 256 * h + 256, state, 1024 * h, 1024 * h + 1024)
        if t < ROUNDS:
            mm(ps(h), 256, "qu", 0, qx, 256 * h)
            act(("bt", 256 * h, 256 * h + 256), (ps(h), 0, 256), ACT.Sign, bias=-(2.0 ** -100))
        else:
            mm(ps(h), 256, "qv", 0, qx, 256 * h)
            act(("yb", 256 * h, 256 * h + 256), (ps(h), 0, 256), ACT.Copy)
            dma("y", "do%d" % h, T.oc[:, 1024 * h:1024 * h + 1024], T[qx][:, 256 * h:256 * h + 256].bitcast(dt.uint8),
                [R(qx, 256 * h, 256 * h + 256)], [])
            dma("s", "dy%d" % h, T.y[:, 256 * h:256 * h + 256], T.yb[:, 256 * h:256 * h + 256],
                [R("yb", 256 * h, 256 * h + 256)], [])

    key_half(0, "xs", 0)
    key_half(0, "xs", 1)
    for t in range(ROUNDS):
        qx, qa, lc = "qx%d" % t, "qa%d" % t, "lc%d" % t
        new = "st%d" % (t + 1)
        quant("qb", 0, 128, "bt", 0, 512)
        mm("ps2", 128, "qb", 0, "qk", 0)
        mm("ps3", 280, "qb", 0, "qk", 32)
        act(("tt", 2, 560, 4), ("ps3", 0, 140), ACT.Copy)
        act(("tt", 3, 560, 4), ("ps3", 140, 280), ACT.Copy)
        for b in range(4):
            mm(ps(6 + b % 2), 512, "qe", 128 * b, qx, 0)
            act(("dd", 512 * b, 512 * b + 512), (ps(6 + b % 2), 0, 512), ACT.Copy, scale=0.5)
        act(("kng",), ("ps2", 3, 32, 4), ACT.Copy, scale=-1.0)
        for h in (0, 1):
            for gg in range(4):
                for b in range(4):
                    c = 4 * (4 * h + gg) + b
                    o = ("ot", 1040 * h + 4 * gg + b, 1040 * h + 1040, 16)
                    if b == 3:
                        act(o, ("kc", 0, 65), ACT.Sign, bias=("kng", c // 4, c // 4 + 1))
                    else:
                        vts(o, ("kc", 0, 65), ("ps2", c, c + 1), 0.5, OP.is_gt, OP.subtract)
            quant("qo", 260 * h, 260 * h + 260, "ot", 1040 * h, 1040 * h + 1040)
        for b in range(4):
            mm("ps3", 128, "qr", 128 * b, "qb", 0)
            act(("kf", b, 512, 4), ("ps3", 0, 128), ACT.Identity, bias=31.5)
        for c in range(5):
            act(("jk", 512 * c, 512 * c + 512), ("kf",), ACT.Sign, bias=("tb", c, c + 1), accum=("acc", c, c + 1))
        act(("b5",), ("acc",), ACT.Copy, bias=256.0, scale=-0.5, lat=0.8)
        dma("y", "dk%d" % t, T.kl[8 * t:8 * t + 8, :], T.kf[0:128:16, :], [R("kf")], [])
        for h in (0, 1):
            for c in range(4):
                p = ps(((0, 1, 4, 5), (0, 1, 4, 2))[h][c])
                mm(p, 256, "ql", 256 + 128 * c, "qo", 260 * h + 4, True, False)
                mm(p, 256, "ql", 768 + 128 * c, "qo", 260 * h, False, True)
                for gg in range(4):
                    k = 12 + 16 * (4 * h + gg) + c
                    if k < VR:
                        vreduce(("rw", k, k + 1), (p, gg, 256, 4), OP.max)
                    else:
                        z = 64 * (2 * c + gg - 2)
                        act(("sj", z, z + 64), (p, gg, 256, 4), ACT.Relu, bias=-512.0, accum=("rw", k, k + 1))
        for o in ("hi", "rv"):
            vts((o, 0, VR), ("rw", 0, VR), M16 - RW, None, OP.add)
            act((o, VR, 140), ("rw", VR, 140), ACT.Identity, bias=M16 - RS)
        vts(("tt", 0, 560, 4), ("hi",), M16, None, OP.subtract)
        vtt(("tt", 1, 560, 4), ("rv",), ("hi",), OP.subtract)
        quant("qt", 0, 140, "tt", 0, 560)
        for q in range(4):
            mm("ps0", 128, "qt", 12 - 4 * q, "ql", 32 * q, q == 0, q == 3)
        for q in range(4):
            mm("ps1", 128, "qt", 12 - 4 * q, "ql", 128 + 32 * q, q == 0, q == 3)
        vts(("po",), ("ps0", 0, 32), 256.0, None, OP.add)
        vts(("ko",), ("ps1", 0, 32), 31.5, None, OP.add)
        msk = "msk%d" % t
        vtt(("em",), ("b5", 1, 5), ("b5", 0, 4), OP.is_equal)
        vtt(("dm",), ("em",), ("dum",), OP.mult)
        vtt(("mk",), ("b5", 0, 4), ("dm",), OP.max)
        vtt(("pk",), ("b5", 1, 5), ("dm",), OP.max)
        vcopy(("mk16",), ("mk",))
        vts(("pk16",), ("pk",), 1.0, None, OP.subtract)
        vscatter((msk,), ("neg",), ("mk16",))
        vscatter(("lsw",), ("vals",), ("po",))
        vtrans(("ltr",), ("lsw",))
        for gg in (0, 1):
            vtt(("lj", 16 * gg, 16 * gg + 16), ("ltr", 16 * gg, 512, 32), ("ltr", 16 * gg + 1, 512, 32), OP.add)
        vtrans(("lk",), ("lj",))
        vcopy(("l16",), ("lk",))
        for b in (0, 2, 1, 3):
            o, i = ("sd", 512 * b, 512 * b + 512), ("dd", 512 * b, 512 * b + 512)
            if b < 2:
                vgather(o, i, ("l16",))
            else:
                act(o, i, ACT.Copy, off=("l16",))
        for b in (0, 2, 1, 3):
            vscan(("sc", 576 * b, 576 * b + 512), (msk, 0, 512), ("sd", 512 * b, 512 * b + 512))
            o, i = ("at", b, 256, 4), ("sc", 576 * b, 576 * b + 576)
            if b < 3:
                act(o, i, ACT.Copy, scale=2.0, off=("pk16",))
            else:
                vts(o, i, 2.0, None, OP.mult, off=("pk16",))
        quant(qa, 0, 128, "at", 0, 512)
        send(t)
        for b in range(4):
            mm(ps(b), 128, "qe", 128 * b, qa, 0)
        for b in range(4):
            act(("own", 64 * b, 64 * b + 64), (ps(b), 0, 64), ACT.Copy)
        if t == 0:
            for b in range(4):
                act(("ebt", 512 * b + b, 512 * b + 512, 4), ("idm",), ACT.Copy, scale=0.5)
            quant("qv", 0, 128, "vs", 0, 512)
            quant("qh", 0, 512, "ebt", 0, 2048)
        for b in (2, 3, 0):
            mm(ps(HB[b]), 512, "qh", 128 * b, qx, 0)
        for b in range(4):
            mm(ps(b), 256, "qe", 128 * b, lc, 0, pre=[("ar%d" % t, arrive(0))])
        for s in range(4):
            for b in range(4):
                o, w = ("mm", 64 * b, 64 * b + 64), ("own" if s == 0 else "mm", 64 * b, 64 * b + 64)
                vtt(o, (ps(b), 64 * s, 64 * s + 64), w, OP.max)
        for b in range(4):
            mm(ps(b), 192, "qe", 128 * b, lc, 256, pre=[("br%d" % t, arrive(1))])
        for s in range(3):
            for b in range(4):
                w = ("mm", 64 * b, 64 * b + 64)
                vtt(("zt", b, 256, 4) if s == 2 else w, (ps(b), 64 * s, 64 * s + 64), w, OP.max)
        quant("qz", 0, 128, "zt", 0, 512)
        for b in range(4):
            mm(ps(b), 128, "qw", 128 * b, "qz", 0)
        for b in range(4):
            vts(("gt", b, 256, 4), (ps(b), 0, 64), 0.0, 0.015625, OP.max, OP.mult)
        quant("qg", 0, 128, "gt", 0, 512)
        for b in (0, 2, 1, 3):
            mm(ps(b), 128, "qe", 128 * b, "qg", 0)
        for b in (0, 2, 1, 3):
            o, i = ("gb", 64 * b, 64 * b + 64), (ps(b), 0, 64)
            if b in (0, 1):
                vts(o, i, 0.5, None, OP.mult)
            else:
                act(o, i, ACT.Copy, scale=0.5)
        for h in (0, 1):
            mine = (2, 3) if h == 0 else (2, 3, 0)
            off = ("ko", 16 * h, 16 * h + 16)
            for b in mine:
                act(("ge", 1024 * h + 256 * b, 1024 * h + 256 * b + 256), ("gb", 64 * b, 64 * b + 64), ACT.Copy, off=off)
            for b in [b for b in range(4) if b not in mine] + list(mine):
                o = (new, 1024 * h + b, 1024 * h + 1024, 4)
                if b in mine:
                    vtt(o, (ps(HB[b]), 256 * h, 256 * h + 256), ("ge", 1024 * h + 256 * b, 1024 * h + 256 * b + 256), OP.add)
                else:
                    vtt(o, ("gb", 64 * b, 64 * b + 64), ("dd", 512 * b + 256 * h, 512 * b + 256 * h + 256), OP.add, off=off)
        for h in (0, 1):
            key_half(t + 1, new, h)

    qx = "qx%d" % ROUNDS
    for k in range(4):
        dma("y", "ds", T.osc[4 * k:4 * k + 4, :], T[qx + "s"][32 * k:32 * k + 4, :], [R(qx)], [])
    if not _PLAN:
        _PLAN.extend(plan(ops, TRIES))
    for i in _PLAN:
        issue(ops[i])
    count["ar0"] = count["ar1"] = arrive(0)
    count["br0"] = count["br1"] = arrive(1)
    for s in SEMAPHORES:
        if count[s]:
            wait("q", s, count[s])
